import numpy as np, ml_dtypes
CORES = [2,6,10,14,18,22,26,30]
N = 8
BF = ml_dtypes.bfloat16
W, L, C, ST, H = 4096, 128, 32, 8, 3
def parts(rng):
    x = rng.integers(0, 256, (N, 8, 16, W)); z = rng.integers(0, 256, (N, 8, 16, L))
    p = rng.integers(0, W, (N, 8, 16, L)); r = rng.integers(0, W, (N, 8, 16, L))
    return x, p, r, z, rng.integers(1000, 1701, (N, 8))
def pack(x, p, r, z, t):
    return {"xt": np.ascontiguousarray(x.reshape(N, 128, W)).astype(np.float32).astype(BF), "pl": np.ascontiguousarray(p.reshape(N, 128, L)).astype(np.int32),
            "pr": np.ascontiguousarray(r.reshape(N, 128, L)).astype(np.int32), "z0": np.ascontiguousarray(z.reshape(N, 128, L)).astype(np.float32).astype(BF),
            "th": np.repeat(t, 16, axis=1).reshape(N, 128, 1).astype(np.int32)}
def setup_inputs(rng):
    return pack(*parts(rng))
def setup_inputs_spread(rng):
    x, p, r, z, t = parts(rng)
    x = np.floor(256 * np.exp2(-8 * rng.random((N, 8, 1, W))) * rng.random((N, 8, 16, W))); z = np.floor(256 * np.exp2(-8 * rng.random((N, 8, 1, L))) * rng.random((N, 8, 16, L)))
    w = []
    for _ in range(2):
        e = rng.choice(np.array([1.0, 2.0, 4.0]), (N, 8, 1, 1)); n = np.minimum(np.floor(W * rng.random((N, 8, 16, L)) ** e), W - 1).astype(np.int64)
        w.append(np.where(rng.random((N, 8, 1, 1)) < 0.5, n, W - 1 - n))
    t = np.minimum(np.floor(4080 * rng.random((N, 8)) ** 3), 4079)
    return pack(np.minimum(x, 255), w[0], w[1], np.minimum(z, 255), t)
def setup_inputs_ends(rng):
    x, p, r, z, t = parts(rng)
    def bits(n):
        v = 255 * rng.integers(0, 2, (N, 8, 16, n)); c = rng.random((N, 8, 1, n))
        return np.where(c < 0.25, 0, np.where(c > 0.75, 255, v))
    x = bits(W); z = bits(L)
    for g in range(8):
        if g in (0, 3, 7): x[:, g, :, 0] = 0
        elif g in (1, 4): x[:, g, :, 0] = 255
        elif g in (2, 5): x[:, g, :, 0] = 0; x[:, g, 15, 0] = 255
        else: x[:, g, :, 0] = 255 * rng.integers(0, 2, (N, 16))
        x[:, g, :, W - 1] = 255 - x[:, g, :, 0]
    p = np.where(rng.random(p.shape) < 0.8, (W - 1) * rng.integers(0, 2, p.shape), p); r = np.where(rng.random(r.shape) < 0.8, (W - 1) * rng.integers(0, 2, r.shape), r)
    t = 4079 * rng.integers(0, 2, (N, 8)); t[:, 0] = 4079; t[:, 7] = 0
    x[:, 7, :, W - 2] = 0; x[:, 7, 15, W - 2] = 255; z[:, 7, :, L - 1] = 0
    r[:, 7, :15, L - 1] = W - 1; r[:, 7, 15, L - 1] = 0; p[:, 7, :15, L - 1] = W - 1; p[:, 7, 15, L - 1] = W - 2
    z[:, 7, :, L - 2] = 0; r[:, 7, :, L - 2] = W - 1; p[:, 7, 0, L - 2] = 0; p[:, 7, 15, L - 2] = W - 1
    z[:, 1, :, 1] = 255; r[:, 1, :, 1] = W - 1; p[:, 1, 0, 1] = 0; p[:, 1, 15, 1] = W - 1
    return pack(x, p, r, z, t)
def setup_inputs_crowd(rng):
    x, p, r, z, t = parts(rng); x[..., 0] = 0; x[..., W - 1] = 255
    q = rng.integers(0, 16, (N, 8, 1, L)); m = (np.arange(16).reshape(1, 1, 16, 1) - q) & 15; lane = np.arange(L)
    b = rng.integers(0, 2, (N, 8, 1, L)); z = np.broadcast_to(255 * b, (N, 8, 16, L))
    far = np.where(rng.random(r.shape) < 0.5, (W - 1) * (1 - b), rng.integers(1, W - 1, r.shape))
    r = np.where(m == 0, (W - 1) * b, far)
    own = (W - 1) * rng.integers(0, 2, (N, 8, 1, L)); e = (m >= 1) & (m < 8)
    e[:, 1::2, :, L - 1] &= m[:, 1::2, :, L - 1] != 7
    e[:, 2] &= (m[:, 2] == 1) & (lane < 32); e[:, 3] &= (m[:, 3] == 1) & (lane < 31); e[:, 6] = False
    p = np.where(e, W - 1 - own, np.where(m < 8, own, p))
    return pack(x, p, r, z, rng.choice(np.array([0, 1000, 1400, 4079]), (N, 8)))
def setup_inputs_ties(rng):
    x, p, r, z, t = parts(rng)
    x = rng.integers(0, 4, x.shape); z = rng.integers(0, 4, z.shape); x[:, 1] += 252; x[:, 6] += 252; z[:, 6] += 252
    same = rng.random((N, 8, 1, L)) < 0.25
    p = np.where(same, np.roll(np.repeat(p[:, :, :4], 4, axis=2), 1, axis=2), p); r = np.where(same, np.tile(r[:, :, :4], (1, 1, 4, 1)), r)
    t = rng.integers(0, 19, (N, 8)); t[:, 3] = 0; near = np.array([3, 5, 7, 9, 19, 21])
    p[:, 3] = W - rng.choice(near, (N, 16, L)); r[:, 3] = W - rng.choice(near, (N, 16, L))
    return pack(x, p, r, z, t)
def setup_inputs_corners(rng):
    x, p, r, z, t = parts(rng); i = np.arange(L).reshape(1, 1, L); j = np.arange(16).reshape(1, 16, 1)
    p[:, 0] = rng.integers(0, W, (N, 16, 1)); r[:, 0] = rng.integers(0, W, (N, 16, 1))
    p[:, 1] = rng.integers(0, W, (N, 1, L)); r[:, 1] = rng.integers(0, W, (N, 1, L))
    p[:, 2] = C * i + (j & (C - 1)); r[:, 2] = C * i + (C - 1 - (j & (C - 1)))
    p[:, 3] = r[:, 3]
    p[:, 4] = ((W - 1) * (np.arange(N) & 1)).reshape(N, 1, 1); r[:, 4] = W - 1 - p[:, 4]
    o = np.argsort(rng.random((N, max(W, 16 * L))), axis=1)[:, :16 * L] & (W - 1)
    p[:, 5] = o.reshape(N, 16, L); r[:, 5] = W - 1 - p[:, 5, ::-1]
    p[:, 6] = C * ((i + 1) % L) + ((j + rng.integers(0, C, (N, 1, 1))) & (C - 1)); r[:, 6] = C * ((i + L - 1) % L) + ((j + rng.integers(0, C, (N, 1, 1))) & (C - 1))
    p[:, 7, :, :L - 1] = ((W - 1) * ((i + j) & 1))[:, :, :L - 1]; r[:, 7, :, :L - 1] = (W - 1) * (j & 1)
    t = rng.choice(np.array([0, 500, 1200, 2000, 4079]), (N, 8)); t[:, 5] = 2048
    z[:, 5] = 255 * rng.integers(0, 2, (N, 1, L)); z[:, 5, :, L - 1] = 0
    x[:, 5, :, 0] = 0; x[:, 5, :, W - 1] = 0; x[:, 5, :8, W - 1] = 255; x[:, 5, 8, W - 1] = 9
    r[:, 5, :8, L - 1] = W - 1; r[:, 5, 15, L - 1] = 0; p[:, 5, :7, L - 1] = W - 1; p[:, 5, 15, L - 1] = 0
    return pack(x, p, r, z, t)
def check_inputs(d):
    bad = []
    for k, lo, hi in (("xt", 0, 255), ("pl", 0, W - 1), ("pr", 0, W - 1), ("z0", 0, 255), ("th", 0, 4079)):
        a = np.asarray(d[k]).astype(np.float64)
        if not (np.min(a) >= lo and np.max(a) <= hi): bad.append("range of " + k)
        if np.any(a != np.floor(a)): bad.append("whole numbers in " + k)
    a = np.asarray(d["th"]).reshape(-1, 16)
    if np.any(a != a[:, :1]): bad.append("the 16 rows of a group in th are alike")
    return bad
def turn(q, s):
    return np.take_along_axis(q, (np.arange(16).reshape(1, 1, 16, 1) + s[:, :, None, :]) & 15, 2)
def items(x, n):
    return np.take_along_axis(x, n.reshape(N, 8, 1, 16 * L), 3).reshape(N, 8, 16, 16, L)
def reference(xt, pl, pr, z0, th):
    x = xt.astype(np.float32).astype(np.int64).reshape(N, 8, 16, W); z = z0.astype(np.float32).astype(np.int64).reshape(N, 8, 16, L)
    p = pl.astype(np.int64).reshape(N, 8, 16, L); r = pr.astype(np.int64).reshape(N, 8, 16, L)
    t = th.astype(np.int64).reshape(N, 8, 16)[:, :, 0]; a = np.zeros((N, 8), np.int64)
    for step in range(ST):
        d = np.add.reduce(np.abs(items(x, r) - z[:, :, :, None, :]), axis=2)
        k = np.argmin(d, axis=2)
        v = items(x, p); y = np.take_along_axis(v, k[:, :, None, None, :], 3)[:, :, :, 0, :]
        f = np.add.reduce(np.abs(v - y[:, :, :, None, :]), axis=2)
        p = turn(p, k); f = turn(f, k); r = turn(r, k + 1); d = turn(d, k + 1)
        lim = (t + (a & 31))[:, :, None, None]; left = f[:, :, 1:8] > lim; right = d[:, :, 1:8] > lim
        p1, p9, r1, r9 = p[:, :, 1:8], p[:, :, 9:16], r[:, :, 1:8], r[:, :, 9:16]
        new = ((p1 * r1 >> 5) + p1 + a[:, :, None, None]) & (W - 1)
        p = np.concatenate([p[:, :, :1], np.where(left, p9, p1), p[:, :, 8:9], np.where(left, new, p9)], axis=2)
        r = np.concatenate([r[:, :, :1], np.where(right, r9, r1), r[:, :, 8:9], np.where(right, r1, r9)], axis=2)
        u = np.add.reduce(y, axis=2)
        np.put_along_axis(x, (C * np.arange(L) + (u & (C - 1)))[:, :, None, :], (y + z) >> 1, 3)
        z = np.abs(y - z)
        if step < ST - 1:
            a = np.add.reduce(left.astype(np.int64), axis=(2, 3))
            p = np.roll(p, H, axis=0); r = np.roll(r, H, axis=0); z = np.roll(z, H, axis=0)
    return {"yx": x.reshape(N, 128, W).astype(np.float32).astype(BF), "yp": p.reshape(N, 128, L).astype(np.float32),
            "yr": r.reshape(N, 128, L).astype(np.float32), "yz": z.reshape(N, 128, L).astype(np.float32).astype(BF)}

@@ -1,0 +1,472 @@
+from concourse.mybir import AluOpType, AxisListType, ActivationFunctionType
+
+ST, HOP, NR = 8, 3, 8
+F32, BF, I32, U16 = "float32", "bfloat16", "int32", "uint16"
+CH = ((0, 512), (512, 1024), (1024, 1536), (1536, 1792), (1792, 2048))
+ORDER = ("s1 wp wr bb szb ee t q4 pl kd val poff sy c7 yoff flag y br ls tr lm loa phigh lo rlow ui ub ua pa d1 uf item uoff "
+         "prod scat fmax sh sm nw d2 lf m1 t2 po cnt").split()
+
+
+def _sb(shape, d):
+    return ("sbuf", [128] + list(shape), d)
+
+
+SCRATCH = {
+    "tab": _sb([4096], BF), "a": _sb([2048], BF), "mx": _sb([2048], BF), "v": _sb([1024], BF), "mf": _sb([1024], BF),
+    "pli": _sb([128], I32), "pri": _sb([128], I32), "thi": _sb([4], I32),
+    "zin": _sb([128 * ST], BF), "zout": _sb([128 * ST], BF), "lin": _sb([192 * ST], BF), "lout": _sb([192 * ST], BF),
+    "pin": _sb([128 * ST], F32), "pout": _sb([128 * ST], F32), "roff": _sb([128 * ST], U16), "rf": _sb([128 * ST], F32),
+    "ai": _sb([144], I32), "ip": _sb([4], I32), "pm": _sb([8], I32), "col": _sb([8], F32), "ti": _sb([128], I32), "lab0": _sb([128], BF),
+    "za": _sb([144], BF), "zm": _sb([144], BF), "idb": _sb([128], BF), "idn": _sb([128], BF), "idh": _sb([128], BF), "id8": _sb([128], BF),
+    "idf": _sb([128], F32), "idnf": _sb([128], F32), "bones": _sb([128], F32),
+    "c8": _sb([128], BF), "cq": _sb([128], BF), "c0": _sb([128], BF), "c4": _sb([128], BF),
+    "rs16": _sb([128], F32), "rs8": _sb([64], F32), "kp16": _sb([128], F32), "kp8": _sb([64], F32),
+    "bc128": _sb([8], U16), "bc64": _sb([8], U16), "tl": _sb([8], U16), "base": _sb([8], F32), "mm8": _sb([64], F32),
+    "pk": _sb([128], F32), "dup": _sb([16, 16], F32), "tr": _sb([256], F32), "wi": _sb([128], I32), "hi3": _sb([16, 8], I32), "lo3": _sb([16, 8], I32),
+    "s1": _sb([128], F32), "szb": _sb([128], F32), "wp": _sb([64], I32), "bb": _sb([64], I32), "ee": _sb([64], I32),
+    "poff": _sb([64], U16), "val": _sb([64], F32), "sy": _sb([64], F32), "yoff": _sb([8], U16), "y": _sb([128], BF),
+    "wr": _sb([128], I32), "q4": _sb([128], I32), "flag": _sb([128], BF), "ls": _sb([128], I32), "lm": _sb([128], I32),
+    "ui": _sb([8], I32), "ua": _sb([8], I32), "uf": _sb([8], F32), "uoff": _sb([8], U16), "item": _sb([128], BF), "ub": _sb([64], F32),
+    "rlow": _sb([8, 16], F32), "prod": _sb([64], I32), "sh": _sb([64], I32), "sm": _sb([64], I32), "nw": _sb([64], I32),
+    "phigh": _sb([64], F32), "d1": _sb([64], F32), "d2": _sb([64], F32), "m1": _sb([64], F32),
+    "cnt": _sb([4], F32), "acv": _sb([4], I32), "a31": _sb([4], I32), "thr": _sb([4], F32), "th1": _sb([4], F32),
+    "sx": _sb([64], I32), "bits": _sb([192], I32), "rn": _sb([128], F32), "xa": _sb([16, 16], F32), "xb": _sb([16, 16], F32),
+    "op": _sb([128], F32), "orr": _sb([128], F32),
+    "pK": ("psum", [128, 512], F32), "pA": ("psum", [128, 32, 16], F32), "pB": ("psum", [128, 32, 16], F32), "pS": ("psum", [128, 512], F32),
+    "pY": ("psum", [128, 512], F32), "pD": ("psum", [128, 512], F32), "pF": ("psum", [128, 512], F32), "pV": ("psum", [128, 512], F32),
+}
+NDMA = 12
+SEMAPHORES = (["cV", "cS", "cP", "cG", "sent"] + ["dm%d" % k for k in range(NDMA)]
+              + ["%s%d" % (n, s) for n in ("az", "al", "ap", "ar") for s in range(1, ST)])
+
+
+def rank_program(g, core, T, topo):
+    rank = T.rank_of(core)
+    if rank is None:
+        return
+    A = AluOpType
+    ACT = ActivationFunctionType
+    queue = {"V": g.vector, "S": g.scalar, "P": g.tensor, "G": g, "Y": g.sync}
+    ops = []
+    writer, readers, banks = {}, {}, {}
+    clock = {q: {} for q in queue}
+    ndma = [0]
+
+    def need(q, dep, waits):
+        if isinstance(dep, tuple):
+            if dep not in clock[q]:
+                clock[q][dep] = True
+                waits.append(dep)
+            return
+        o = ops[dep]
+        if o["q"] == "P" and q == "P":
+            return
+        if clock[q].get(o["q"], -1) >= dep:
+            return
+        waits.append(dep)
+        o["used"] = True
+        for k, val in o["clock"].items():
+            if isinstance(k, tuple):
+                clock[q][k] = True
+            elif clock[q].get(k, -1) < val:
+                clock[q][k] = val
+        clock[q][o["q"]] = dep
+
+    def op(q, fn, r=(), w=(), kind="c"):
+        deps = []
+        for k in r:
+            if k in writer:
+                deps.append(writer[k])
+        for k in w:
+            if k in writer:
+                deps.append(writer[k])
+            deps.extend(readers.get(k, []))
+        bk = set(k.split(":")[0] for k in list(r) + list(w) if ":" in k)
+        for b in bk:
+            for e, i in banks.get(b, {}).items():
+                if e != q:
+                    deps.append(i)
+        waits = []
+        for d in sorted([d for d in deps if not isinstance(d, tuple)], reverse=True) + [d for d in deps if isinstance(d, tuple)]:
+            need(q, d, waits)
+        idx = len(ops)
+        tok = idx
+        if kind == "dma":
+            tok = ("dm%d" % ndma[0], 16)
+            ndma[0] += 1
+        ops.append({"q": q, "fn": fn, "waits": waits, "kind": kind, "used": False, "clock": dict(clock[q]), "tok": tok})
+        if kind != "send":
+            for k in r:
+                readers.setdefault(k, []).append(tok)
+        for k in w:
+            writer[k] = tok
+            readers[k] = []
+        for b in bk:
+            banks.setdefault(b, {})[q] = idx
+        return tok
+
+    def tt(out, a, b, o, r, w):
+        op("V", lambda: g.vector.tensor_tensor(out, a, b, o), r, w)
+
+    def ts(out, a, s1, s2, o0, o1, r, w):
+        if o1 is None:
+            op("V", lambda: g.vector.tensor_scalar(out, a, s1, None, o0), r, w)
+        else:
+            op("V", lambda: g.vector.tensor_scalar(out, a, s1, s2, o0, o1), r, w)
+
+    def cp(out, a, r, w):
+        op("V", lambda: g.vector.tensor_copy(out, a), r, w)
+
+    def scan(out, d0, d1, o0, o1, r, w):
+        op("V", lambda: g.vector.tensor_tensor_scan(out, d0, d1, 0.0, o0, o1), r, w)
+
+    def ms(ap, c, w):
+        op("V", lambda: g.vector.memset(ap, c), (), w)
+
+    def mm(out, l, rh, st, sp, r, w):
+        op("P", lambda: g.tensor.matmul(out, l, rh, st, sp), r, w)
+
+    def act(out, a, f, r, w, scale=1.0):
+        op("S", lambda: g.scalar.activation(out, a, f, scale=scale), r, w)
+
+    def dma(q, out, a, r, w):
+        return op(q, lambda: queue[q].dma_start(out, a), r, w, kind="dma")
+
+    sent = [0]
+
+    def send(dst_rank, out, a, sem, r):
+        dst = T.cores[dst_rank]
+        rid, pid, _ = topo.addr(dst)
+        m = topo.mask(core, dst)
+        sent[0] += len(topo.engines(core, dst))
+        op("G", lambda: g.remote_dma(out, a, T.sem[sem], T.sem.sent, pid, rid, m), r, (), kind="send")
+
+    def lands(src_rank, calls):
+        return calls * len(topo.engines(T.cores[src_rank], core))
+
+    def blk(t, s, n, a=0, b=None):
+        return t[:, n * s + a:n * s + (n if b is None else b)]
+
+    prev, nxt = (rank - HOP) % NR, (rank + HOP) % NR
+    for s in range(1, ST):
+        writer["z%d" % s] = ("az%d" % s, lands(prev, 1))
+        writer["l%d" % s] = ("al%d" % s, lands(prev, 1))
+        writer["p%d" % s] = ("ap%d" % s, lands(prev, 1))
+        writer["ro%d" % s] = writer["rf%d" % s] = ("ar%d" % s, lands((rank - HOP * s) % NR, 2))
+
+    dma("Y", T.pri[:], T.pr[:], (), ["pri"])
+    dma("Y", T.pli[:], T.pl[:], (), ["pli"])
+    dma("S", T.tab[:], T.xt[:], (), ["tab"])
+    dma("Y", blk(T.zin, 0, 128), T.z0[:], (), ["z0"])
+    dma("Y", T.thi[:, 0:1], T.th[:], (), ["thi"])
+
+    op("G", lambda: g.iota(T.ip[:, 0:1], [[0, 1]], 0, 1), (), ["ip"])
+    op("G", lambda: g.iota(T.ai[:], [[1, 144]], 0, 0), (), ["ai"])
+    op("G", lambda: g.iota(T.lab0[:], [[0, 8], [1, 8], [8, 2]], 0, 0, allow_small_or_imprecise_dtypes=True), (), ["lab0"])
+    BIG = 1.0e29
+    for t, c in (("c8", -8192.0), ("cq", -0.25), ("c0", 0.0), ("c4", 4096.0)):
+        ms(T[t][:], c, [t])
+    masks = (("rs16", 16, -BIG, BIG), ("rs8", 8, -BIG, BIG), ("kp16", 16, 0.0, 1.0), ("kp8", 8, 0.0, 1.0))
+    for t, n, lo, hi in masks:
+        ms(T[t][:], hi, [t])
+    for t, n, lo, hi in masks:
+        ms(T[t][:, 0::n], lo, [t])
+    ms(T.a31[:, 0:1], 0, ["a31"])
+    for k, m in enumerate((31, 112, 8, 15)):
+        ts(T.pm[:, k:k + 1], T.ip[:, 0:1], m, None, A.bitwise_and, None, ["ip"], ["pm%d" % k])
+    cp(T.col[:, 0:1], T.pm[:, 0:1], ["pm0"], ["col0"])
+    cp(T.col[:, 1:2], T.pm[:, 1:2], ["pm1"], ["col1"])
+    ts(T.col[:, 2:3], T.pm[:, 1:2], 15.0, None, A.add, None, ["pm1"], ["col2"])
+    ts(T.col[:, 3:4], T.pm[:, 2:3], 2.0, 15.0, A.mult, A.add, ["pm2"], ["col3"])
+    ts(T.col[:, 4:5], T.pm[:, 3:4], 32.0, None, A.mult, None, ["pm3"], ["col4"])
+    cp(T.col[:, 5:6], T.ip[:, 0:1], ["ip"], ["col5"])
+    ts(T.tl[:], T.ai[:, 0:8], 32.0, T.col[:, 0:1], A.mult, A.add, ["ai", "col0"], ["tl"])
+    ts(T.idb[:], T.ai[:, 0:128], T.col[:, 5:6], None, A.is_equal, None, ["ai", "col5"], ["idb"])
+    ts(T.za[:], T.ai[:], T.col[:, 2:3], 65536.0, A.is_equal, A.mult, ["ai", "col2"], ["za"])
+    ts(T.zm[:], T.ai[:], T.col[:, 2:3], -131072.0, A.is_equal, A.mult, ["ai", "col2"], ["zm"])
+
+    ts(T.pk[:], T.pli[:], 4096.0, None, A.mult, None, ["pli"], ["pk"])
+    for e in range(2):
+        tt(T.dup[:, e::2, :], T.pk[:], T.pri[:], A.add, ["pk", "pri"], ["dup%d" % e])
+    op("V", lambda: g.vector.transpose(T.tr[:], T.dup[:]), ["dup0", "dup1"], ["tr"])
+    cp(T.wi[:], T.tr[:, :].indirect(T.tl[:, 0:8]), ["tr", "tl"], ["wi"])
+    ts(T.lo3[:], T.wi[:], 4095, None, A.bitwise_and, None, ["wi"], ["lo3"])
+    ts(T.hi3[:], T.wi[:], 12, None, A.arith_shift_right, None, ["wi"], ["hi3"])
+    for h in range(2):
+        cp(T.roff[:, 64 * h:64 * h + 64], T.lo3[:, h::2, :], ["lo3"], ["ro0h%d" % h])
+    cp(T.rf[:, 0:64], T.lo3[:, 0::2, :], ["lo3"], ["rf0a"])
+    tt(T.rf[:, 64:128], T.lo3[:, 1::2, :], T.lo3[:, 0::2, :], A.subtract, ["lo3"], ["rf0"])
+    for h in range(2):
+        cp(T.pin[:, 64 * h:64 * h + 64], T.hi3[:, h::2, :], ["hi3"], ["p0" if h else "p0a"])
+    writer["ro0"] = writer["ro0h1"]
+
+    for t, wgt in (("idn", -1.0), ("idf", 1.0), ("idnf", -1.0), ("idh", 0.5), ("id8", 32768.0)):
+        ts(T[t][:], T.ai[:, 0:128], T.col[:, 5:6], wgt, A.is_equal, A.mult, ["ai", "col5"], [t])
+    ts(T.bc128[:], T.ai[:, 0:8], 16.0, 15.0, A.mult, A.add, ["ai"], ["bc128"])
+    ts(T.bc64[:], T.ai[:, 0:8], 32.0, T.col[:, 3:4], A.mult, A.add, ["ai", "col3"], ["bc64"])
+    ts(T.base[:], T.ai[:, 0:8], 512.0, T.col[:, 4:5], A.mult, A.add, ["ai", "col4"], ["base"])
+    ts(T.ti[:], T.ai[:, 0:128], 112, None, A.bitwise_and, None, ["ai"], ["ti"])
+    ts(T.sx[:], T.ai[:, 0:64], 7, None, A.bitwise_and, None, ["ai"], ["sx"])
+    ts(T.bones[:], T.ti[:], T.col[:, 1:2], None, A.is_equal, None, ["ti", "col1"], ["bones"])
+    ts(T.lin[:, 0:128], T.lab0[:], 4096.0, None, A.mult, None, ["lab0"], ["l0a"])
+    ts(T.lin[:, 128:192], T.sx[:], 2.0, 4096.0, A.add, A.mult, ["sx"], ["l0"])
+    ts(T.th1[:, 0:1], T.thi[:, 0:1], 1.125, None, A.add, None, ["thi"], ["th1"])
+    ts(T.mm8[:], T.sx[:], 8.0, 4096.0, A.add, A.mult, ["sx"], ["mm8"])
+
+    def sel(t, r):
+        return t[:, 15 - r:143 - r]
+
+    K, SZ, U, AP_ = T.pK[:, 0:128], T.pS[:, 0:128], T.pS[:, 128:192], T.pS[:, 192:193]
+    R8, HF, Dp, DP, Fp = T.pF[:, 128:256], T.pY[:, 128:256], T.pD[:, 0:128], T.pD[:, 128:192], T.pF[:, 0:64]
+    tP, PL, C7, bR, tR, LF, PA = (T.pV[:, 0:64], T.pV[:, 64:128], T.pV[:, 128:256], T.pV[:, 256:320], T.pV[:, 320:384],
+                                  T.pV[:, 384:448], T.pV[:, 448:512])
+    tiles = ((T.pA, "pA:t"), (T.pB, "pB:t"))
+    win = T.tab[:, :]
+    outs = []
+
+    def tile(hh, src, key):
+        for m in range(8):
+            mm(tiles[hh][0][:, m::8, :], T.idb[:], src, True, True, ["idb", key], [tiles[hh][1]])
+
+    def send_r(s):
+        d = (rank + HOP * s) % NR
+        send(d, blk(T.roff, s, 128), blk(T.roff, 0, 128), "ar%d" % s, ["ro0h0", "ro0h1"])
+        send(d, blk(T.rf, s, 128), blk(T.rf, 0, 128), "ar%d" % s, ["rf0a", "rf0"])
+
+    def gather_r(s):
+        for k, (lo_, hi_) in enumerate(CH):
+            src = win.indirect(blk(T.roff, s, 128, lo_ // 16, hi_ // 16))
+            if s == 0 and k >= 3:
+                cp(T.a[:, lo_:hi_], src, ["tab", "ro%d" % s], ["a%d" % k])
+            else:
+                act(T.a[:, lo_:hi_], src, ACT.Copy, ["tab", "ro%d" % s], ["a%d" % k])
+
+    def ztiles(s):
+        for hh in range(2):
+            if hh == 0:
+                mm(K, T.idb[:], T.c8[:], True, False, ["idb", "c8"], ["pK:k"])
+            tile(hh, blk(T.zin, s, 128, 64 * hh, 64 * hh + 64), "z%d" % s)
+
+    def nearest(s):
+        for r in range(16):
+            mm(T.pK[:, 0:128:2], sel(T.za, r), T.a[:, r:1024:16], False, False, ["a0", "a1"], ["pK:k"])
+
+        for k in ((3, 4, 0, 1, 2) if s == 0 else range(5)):
+            lo_, hi_ = CH[k]
+            t = tiles[lo_ // 512 % 2]
+            tt(T.mx[:, lo_:hi_], T.a[:, lo_:hi_], t[0][:, lo_ % 512 // 16:(hi_ - 1) % 512 // 16 + 1, :], A.max, ["a%d" % k, t[1]], ["mx%d" % k])
+        for r in range(16):
+            mm(T.pK[:, 0:128:2], sel(T.zm, r), T.mx[:, r:1024:16], False, False, ["zm", "mx0", "mx1"], ["pK:k"])
+        mm(K, T.idn[:], blk(T.lin, s, 192, 0, 128), False, False, ["idn", "l%d" % s], ["pK:k"])
+        for r in range(16):
+            mm(T.pK[:, 1:128:2], sel(T.za, r), T.a[:, 1024 + r:2048:16], False, False, ["a2", "a3", "a4"], ["pK:k"])
+        for r in range(16):
+            mm(T.pK[:, 1:128:2], sel(T.zm, r), T.mx[:, 1024 + r:2048:16], False, r == 15, ["mx2", "mx3", "mx4"], ["pK:k"])
+        if s:
+            cp(T.acv[:, 0:1], AP_, ["pS:a"], ["acv"])
+            ts(T.a31[:, 0:1], T.acv[:, 0:1], 31, None, A.bitwise_and, None, ["acv"], ["a31"])
+        ts(T.thr[:, 0:1], T.a31[:, 0:1], T.th1[:, 0:1], -65536.0, A.add, A.mult, ["a31", "th1"], ["thr"])
+        mm(SZ, T.idb[:], T.c0[:], True, False, ["c0"], ["pS:sz"])
+        for r in range(16):
+            mm(T.pS[:, 0:128:16], sel(T.za, r), T.zin[:, 128 * s + r:128 * s + 128:16], False, r == 15, ["za"], ["pS:sz"])
+        mm(DP, T.idf[:], blk(T.pin, s, 128, 64, 128), True, False, ["idf", "p%d" % s], ["pD:dp"])
+        mm(DP, T.idnf[:], blk(T.pin, s, 128, 0, 64), False, True, ["idnf", "p%d" % s], ["pD:dp"])
+
+
+    def step(s):
+        last = s == ST - 1
+        z, zk, lk, pk_, rk = blk(T.zin, s, 128), "z%d" % s, "l%d" % s, "p%d" % s, "rf%d" % s
+        plo, phi = blk(T.pin, s, 128, 0, 64), blk(T.pin, s, 128, 64, 128)
+        rlo, dr = blk(T.rf, s, 128, 0, 64), blk(T.rf, s, 128, 64, 128)
+        k = (s + 1) % 8
+
+        def poff():
+            cp(T.poff[:], PL, ["pV:pl"], ["poff"])
+            act(T.v[:, 0:512], win.indirect(T.poff[:, 0:32]), ACT.Copy, ["tab", "poff"], ["v0"])
+
+        def flag():
+            tt(T.flag[:], T.q4[:], C7, A.is_lt, ["q4", "pV:c7"], ["flag"])
+            mm(R8, T.idb[:], T.c4[:], True, False, ["c4"], ["pF:r8"])
+            mm(R8, T.id8[:], T.flag[:], False, False, ["id8", "flag"], ["pF:r8"])
+            mm(T.pF[:, 128:256:2], T.id8[:], T.flag[:, 1::2], False, False, ["flag"], ["pF:r8"])
+            mm(T.pF[:, 129:256:2], T.id8[:], T.flag[:, 0::2], False, True, ["flag"], ["pF:r8"])
+
+        def y():
+            cp(T.y[:], win.indirect(T.yoff[:, 0:8]), ["tab", "yoff"], ["y"])
+            mm(Dp, T.idb[:], T.y[:], True, False, ["y"], ["pD:d"])
+            mm(Dp, T.idn[:], z, False, True, [zk], ["pD:d"])
+            act(blk(T.zout, s, 128), Dp, ACT.Abs, ["pD:d"], ["zo%d" % s])
+            if last:
+                outs.append(dma("Y", T.yz[:], blk(T.zout, s, 128), ["zo%d" % s], ()))
+            else:
+                send(nxt, blk(T.zin, s + 1, 128), blk(T.zout, s, 128), "az%d" % (s + 1), ["zo%d" % s])
+            act(T.v[:, 512:1024], win.indirect(T.poff[:, 32:64]), ACT.Copy, ["tab", "poff"], ["v1"])
+            mm(U, T.idb[:], T.c0[:, 0:64], True, False, [], ["pS:u"])
+            for r in range(16):
+                mm(T.pS[:, 128:192:8], sel(T.za, r), T.y[:, r::16], False, r == 15, ["y"], ["pS:u"])
+            mm(HF, T.idh[:], T.y[:], True, False, ["idh", "y"], ["pY:h"])
+            mm(HF, T.idh[:], z, False, False, [zk], ["pY:h"])
+            mm(HF, T.idb[:], T.cq[:], False, True, ["cq"], ["pY:h"])
+            mm(T.pA[:], T.idb[:], T.v[:, 0:512], True, False, ["v0"], ["pA:t"])
+            for m in range(8):
+                mm(T.pA[:, m::8, :], T.idn[:], T.y[:, 0:64], False, m == 7, ["y"], ["pA:t"])
+            act(T.mf[:, 0:512], T.pA[:], ACT.Abs, ["pA:t"], ["mf0"], 0.5)
+            tile(1, T.y[:, 64:128], "y")
+
+        def rlow():
+            tt(T.rlow[:, :, 0:8], rlo, tR, A.add, [rk, "pV:tr"], ["rlowa"])
+            if k:
+                tt(T.rlow[:, :, 8:16], rlo, tR, A.add, [rk, "pV:tr"], ["rlowb"])
+
+        def ub():
+            scan(T.ub[:, 32:64], T.kp8[:, 32:64], T.pS[:, 160:192], A.mult, A.add, ["kp8", "pS:u"], ["ub"])
+            mm(Fp, T.idb[:], T.c8[:, 0:64], True, False, [], ["pF:f"])
+            mm(T.pF[:, 32:64], T.idf[:], T.ub[:, 32:64], False, False, ["ub"], ["pF:f"])
+            for r in range(16):
+                mm(T.pF[:, 32:64], sel(T.za, r), T.v[:, 512 + r:1024:16], False, False, ["v1"], ["pF:f"])
+
+        def lo():
+            ts(blk(T.lout, s, 192, 0, 128), T.lm[:], 0.0, None, A.add, None, ["lm"], ["lo%d" % s])
+            send(nxt, blk(T.lin, s + 1, 192), blk(T.lout, s, 192), "al%d" % (s + 1), ["loa%d" % s, "lo%d" % s])
+
+        def scat():
+            cp(win.indirect(T.uoff[:, 0:8]), T.item[:], ["uoff", "item"], ["tab"])
+            if last:
+                outs.append(dma("S", T.yx[0:64, :], T.tab[0:64, :], ["tab"], ()))
+                outs.append(dma("Y", T.yx[64:128, :], T.tab[64:128, :], ["tab"], ()))
+            else:
+                gather_r(s + 1)
+
+        def fmax():
+            tt(T.mf[:, 512:1024], T.v[:, 512:1024], T.pB[:], A.max, ["v1", "pB:t"], ["mf1"])
+            for r in range(16):
+                mm(Fp, sel(T.zm, r), T.mf[:, r::16], False, r == 15, ["mf0", "mf1"], ["pF:f"])
+            if not last:
+                ztiles(s + 1)
+
+        def po():
+            tt(blk(T.pout, s, 128, 0, 64), T.m1[:], PL, A.add, ["m1", "pV:pl"], ["poa%d" % s])
+            tt(blk(T.pout, s, 128, 64, 128), T.phigh[:], tR, A.add, ["phigh", "pV:tr"], ["po%d" % s])
+            if not last:
+                send(nxt, blk(T.pin, s + 1, 128), blk(T.pout, s, 128), "ap%d" % (s + 1), ["poa%d" % s, "po%d" % s])
+                if s + 2 < ST:
+                    send_r(s + 2)
+
+        def cnt():
+            op("V", lambda: g.vector.tensor_reduce(T.cnt[:, 0:1], LF, AxisListType.X, A.add), ["pV:lf"], ["cnt"])
+            mm(AP_, T.bones[:], T.cnt[:, 0:1], True, True, ["bones", "cnt"], ["pS:a"])
+
+        call = {
+            "s1": lambda: scan(T.s1[:], T.rs16[:], K, A.min, A.max, ["rs16", "pK:k"], ["s1"]),
+            "wp": lambda: tt(T.wp[:], T.s1[:, :].indirect(T.bc64[:, 0:4]), blk(T.lin, s, 192, 128, 192), A.add, ["s1", "bc64", lk], ["wp"]),
+            "bb": lambda: ts(T.bb[:], T.wp[:], 15, 1, A.arith_shift_right, A.bitwise_and, ["wp"], ["bb"]),
+            "ee": lambda: ts(T.ee[:], T.wp[:], 7 << 12, None, A.bitwise_and, None, ["wp"], ["ee"]),
+            "t": lambda: tt(tP, T.bb[:], DP, A.mult, ["bb", "pD:dp"], ["pV:t"]),
+            "pl": lambda: tt(PL, plo, tP, A.add, [pk_, "pV:t"], ["pV:pl"]),
+            "poff": poff,
+            "val": lambda: tt(T.val[:], PL, T.ee[:], A.subtract, ["pV:pl", "ee"], ["val"]),
+            "sy": lambda: scan(T.sy[:], T.rs8[:], T.val[:], A.min, A.max, ["rs8", "val"], ["sy"]),
+            "yoff": lambda: cp(T.yoff[:], T.sy[:, 7::8], ["sy"], ["yoff"]),
+            "y": y,
+            "szb": lambda: scan(T.szb[:], T.kp16[:], SZ, A.mult, A.add, ["kp16", "pS:sz"], ["szb"]),
+            "kd": lambda: tt(C7, K, T.szb[:], A.add, ["pK:k", "szb"], ["pV:c7"]),
+            "c7": lambda: ts(C7, C7, T.thr[:, 0:1], 7.0 * 4096, A.is_le, A.mult, ["pV:c7", "thr"], ["pV:c7"]),
+            "wr": lambda: tt(T.wr[:], T.s1[:, :].indirect(T.bc128[:, 0:8]), blk(T.lin, s, 192, 0, 128), A.add, ["s1", "bc128", lk], ["wr"]),
+            "q4": lambda: ts(T.q4[:], T.wr[:], 15 << 12, None, A.bitwise_and, None, ["wr"], ["q4"]),
+            "flag": flag,
+            "ls": lambda: tt(T.ls[:], T.q4[:], R8, A.add, ["q4", "pF:r8"], ["ls"]),
+            "loa": lambda: ts(blk(T.lout, s, 192, 128, 192), T.ee[:], 8192.0, None, A.add, None, ["ee"], ["loa%d" % s]),
+            "lm": lambda: ts(T.lm[:], T.ls[:], 15 << 12, None, A.bitwise_and, None, ["ls"], ["lm"]),
+            "lo": lo,
+            "ui": lambda: cp(T.ui[:], T.pS[:, 128:192:8], ["pS:u"], ["ui"]),
+            "ua": lambda: ts(T.ua[:], T.ui[:], 16, 31, A.arith_shift_right, A.bitwise_and, ["ui"], ["ua"]),
+            "uf": lambda: tt(T.uf[:], T.ua[:], T.base[:], A.add, ["ua", "base"], ["uf"]),
+            "uoff": lambda: cp(T.uoff[:], T.uf[:], ["uf"], ["uoff"]),
+            "item": lambda: ts(T.item[:], HF, 12582912.0, 12582912.0, A.add, A.subtract, ["pY:h"], ["item"]),
+            "ub": ub, "scat": scat, "fmax": fmax,
+            "phigh": lambda: tt(T.phigh[:], phi, tP, A.subtract, [pk_, "pV:t"], ["phigh"]),
+            "br": lambda: ts(bR, T.q4[:, 0::2], 32768.0, None, A.is_ge, None, ["q4"], ["pV:br"]),
+            "tr": lambda: tt(tR, dr, bR, A.mult, [rk, "pV:br"], ["pV:tr"]),
+            "d1": lambda: tt(T.d1[:], T.phigh[:], PL, A.subtract, ["phigh", "pV:pl"], ["d1"]),
+            "rlow": rlow,
+            "pa": lambda: ts(PA, PL, AP_, None, A.add, None, ["pV:pl", "pS:a"], ["pV:pa"]),
+            "prod": lambda: tt(T.prod[:], T.rlow[:, :, k:k + 8], PL, A.mult, ["rlowa", "rlowb", "pV:pl"], ["prod"]),
+            "sh": lambda: ts(T.sh[:], T.prod[:], 5, None, A.arith_shift_right, None, ["prod"], ["sh"]),
+            "sm": lambda: tt(T.sm[:], T.sh[:], PA if s else PL, A.add, ["sh", "pV:pa", "pV:pl"], ["sm"]),
+            "nw": lambda: ts(T.nw[:], T.sm[:], 4095, None, A.bitwise_and, None, ["sm"], ["nw"]),
+            "d2": lambda: tt(T.d2[:], T.nw[:], T.phigh[:], A.subtract, ["nw", "phigh"], ["d2"]),
+            "lf": lambda: ts(LF, Fp, T.thr[:, 0:1], None, A.is_le, None, ["pF:f", "thr"], ["pV:lf"]),
+            "m1": lambda: tt(T.m1[:], T.d1[:], LF, A.mult, ["d1", "pV:lf"], ["m1"]),
+            "t2": lambda: tt(tR, T.d2[:], LF, A.mult, ["d2", "pV:lf"], ["pV:tr"]),
+            "po": po, "cnt": cnt,
+        }
+        skip = (("loa", "lm", "lo", "cnt") if last else ()) + (("pa",) if s == 0 else ())
+        for n in ORDER:
+            if n not in skip:
+                call[n]()
+
+    send_r(1)
+    gather_r(0)
+    ztiles(0)
+    for s in range(ST):
+        nearest(s)
+        step(s)
+
+    s = ST - 1
+    rlo, dr = blk(T.rf, s, 128, 0, 64), blk(T.rf, s, 128, 64, 128)
+    ts(T.bb[:], T.ls[:, 0::2], 15, 1, A.arith_shift_right, A.bitwise_and, ["ls"], ["bb"])
+    tt(T.sx[:], T.mm8[:], T.ee[:], A.subtract, ["mm8", "ee"], ["sx"])
+    ts(T.pk[:], blk(T.pout, s, 128), 4096.0, None, A.mult, None, ["poa7", "po7"], ["pk"])
+    tt(tP, T.bb[:], dr, A.mult, ["bb"], ["pV:t"])
+    tt(T.d1[:], rlo, dr, A.add, [], ["d1"])
+    for b in range(3):
+        ts(T.bits[:, 64 * b:64 * b + 64], T.sx[:], 12 + b, 1, A.arith_shift_right, A.bitwise_and, ["sx"], ["bits%d" % b])
+    tt(T.pV[:, 128:192], rlo, tP, A.add, ["pV:t"], ["pV:c7"])
+    tt(T.pV[:, 192:256], T.d1[:], tP, A.subtract, ["d1", "pV:t"], ["pV:c7b"])
+    cur, ck, oth, ok = T.xa, "xa", T.xb, "xb"
+    for e in range(2):
+        tt(cur[:, :, 8 * e:8 * e + 8], T.pk[:], C7, A.add, ["pk", "pV:c7", "pV:c7b"], [ck + str(e)])
+    for b in range(3):
+        k = 1 << b
+        tt(T.pV[:, 0:128], cur[:, :, k:k + 8], cur[:, :, 0:8], A.subtract, [ck + "0", ck + "1"], ["pV:t", "pV:pl"])
+        for h in range(2):
+            tt(T.pV[:, 256 + 64 * h:320 + 64 * h], T.pV[:, 64 * h:64 * h + 64], T.bits[:, 64 * b:64 * b + 64], A.mult,
+               ["pV:t", "bits%d" % b], ["pV:tr" if h else "pV:br"])
+        if b < 2:
+            for e in range(2):
+                tt(oth[:, :, 8 * e:8 * e + 8], cur[:, :, 0:8], T.pV[:, 256:384], A.add, [ck + "0", "pV:br", "pV:tr"], [ok + str(e)])
+            cur, ck, oth, ok = oth, ok, cur, ck
+        else:
+            for e in range(2):
+                for h in range(2):
+                    tt(T.dup[:, e::2, 8 * h:8 * h + 8], cur[:, 8 * h:8 * h + 8, 0:8], T.pV[:, 256 + 64 * h:320 + 64 * h], A.add,
+                       [ck + "0", "pV:br", "pV:tr"], ["fin%d%d" % (e, h)])
+    op("V", lambda: g.vector.transpose(T.tr[:], T.dup[:]), ["fin00", "fin01", "fin10", "fin11"], ["tr"])
+    cp(T.wi[:], T.tr[:, :].indirect(T.tl[:, 0:8]), ["tr"], ["wi"])
+    ts(T.hi3[:], T.wi[:], 12, None, A.arith_shift_right, None, ["wi"], ["hi3"])
+    ts(T.lo3[:], T.wi[:], 4095, None, A.bitwise_and, None, ["wi"], ["lo3"])
+    cp(T.op[:], T.hi3[:], ["hi3"], ["op"])
+    outs.append(dma("Y", T.yp[:], T.op[:], ["op"], ()))
+    cp(T.orr[:], T.lo3[:], ["lo3"], ["orr"])
+    outs.append(dma("S", T.yr[:], T.orr[:], ["orr"], ()))
+
+    count = {q: 0 for q in queue}
+    for o in ops:
+        if o["kind"] == "c" and o["used"]:
+            count[o["q"]] += 1
+            o["n"] = count[o["q"]]
+    for o in ops:
+        e = queue[o["q"]]
+        for d in o["waits"]:
+            if isinstance(d, tuple):
+                e.wait_ge(T.sem[d[0]], d[1])
+            else:
+                e.wait_ge(T.sem["c" + ops[d]["q"]], ops[d]["n"])
+        ins = o["fn"]()
+        if o["kind"] == "dma":
+            ins.then_inc(T.sem[o["tok"][0]], 16)
+        elif o["kind"] == "c" and o["used"]:
+            ins.then_inc(T.sem["c" + o["q"]], 1)
+    for tok in outs:
+        g.wait_ge(T.sem[tok[0]], tok[1])
+    g.wait_ge(T.sem.sent, sent[0])

@@ -1,10 +1,15 @@
-from concourse.mybir import AluOpType, AxisListType, ActivationFunctionType
+from concourse.mybir import AluOpType, ActivationFunctionType
+from concourse.bass import DstId, RemoteDMATransfer
 
 ST, HOP, NR = 8, 3, 8
-F32, BF, I32, U16 = "float32", "bfloat16", "int32", "uint16"
-CH = ((0, 512), (512, 1024), (1024, 1536), (1536, 1792), (1792, 2048))
-ORDER = ("s1 wp wr bb szb ee t q4 pl kd val poff sy c7 yoff flag y br ls tr lm loa phigh lo rlow ui ub ua pa d1 uf item uoff "
-         "prod scat fmax sh sm nw d2 lf m1 t2 po cnt").split()
+F32, BF, F16, I32, U16 = "float32", "bfloat16", "float16", "int32", "uint16"
+AW = 136
+CH = (("S", 0, 32), ("V", 32, 48), ("V", 48, 64), ("S", 64, 96), ("S", 96, 112), ("S", 112, 128))
+MX = ((0, 32, 0, 1), (32, 64, 0, 1), (64, 96, 0, 2), (96, 128, 0, 2), (64, 96, 1, 2), (96, 128, 1, 2))
+ORDER = ("s1 wp keep bb sy t8 t thrb yoff y zd pl wr u plu poff q4 h far n16 tr v0 fd0 jn zabs zsend v1 hf pa qi rlow ph phu fr prod flag fa2 sh "
+         "fa0 fd1 uoff fa1 item d1 r8 scat init fa3 sm lo nw lsend fsa g2 d2 fsb zt1 lf g1 m1 m2 zt0 g3 x2 po rsend g5 g4 sa1 x3 sm1 g0 sa0 sg x1 "
+         "cnt xx qb x0 x5 lab x4 sm0 sm2 sl thr af dp dl").split()
+FIRST = "g0 g1 g2 init zt0 zt1 lab sg sl dl dp g3 g4 x0 x1 sa0 sm0 g5 sa1 x2 x3 sm1 x4 x5 sm2".split()
 
 
 def _sb(shape, d):
@@ -12,32 +17,34 @@ def _sb(shape, d):
 
 
 SCRATCH = {
-    "tab": _sb([4096], BF), "a": _sb([2048], BF), "mx": _sb([2048], BF), "v": _sb([1024], BF), "mf": _sb([1024], BF),
+    "tab": _sb([4096], BF), "a": _sb([AW * 8 * 16], BF), "mx": _sb([128, 16], BF), "v": _sb([1024], BF), "mf": _sb([64, 16], BF),
     "pli": _sb([128], I32), "pri": _sb([128], I32), "thi": _sb([4], I32),
-    "zin": _sb([128 * ST], BF), "zout": _sb([128 * ST], BF), "lin": _sb([192 * ST], BF), "lout": _sb([192 * ST], BF),
-    "pin": _sb([128 * ST], F32), "pout": _sb([128 * ST], F32), "roff": _sb([128 * ST], U16), "rf": _sb([128 * ST], F32),
-    "ai": _sb([144], I32), "ip": _sb([4], I32), "pm": _sb([8], I32), "col": _sb([8], F32), "ti": _sb([128], I32), "lab0": _sb([128], BF),
-    "za": _sb([144], BF), "zm": _sb([144], BF), "idb": _sb([128], BF), "idn": _sb([128], BF), "idh": _sb([128], BF), "id8": _sb([128], BF),
-    "idf": _sb([128], F32), "idnf": _sb([128], F32), "bones": _sb([128], F32),
-    "c8": _sb([128], BF), "cq": _sb([128], BF), "c0": _sb([128], BF), "c4": _sb([128], BF),
-    "rs16": _sb([128], F32), "rs8": _sb([64], F32), "kp16": _sb([128], F32), "kp8": _sb([64], F32),
-    "bc128": _sb([8], U16), "bc64": _sb([8], U16), "tl": _sb([8], U16), "base": _sb([8], F32), "mm8": _sb([64], F32),
+    "zout": _sb([128 * 8], BF), "lin": _sb([128 * 8], BF), "lout": _sb([128 * 8], BF), "jin": _sb([64 * 8], I32), "jout": _sb([64 * 8], I32),
+    "pin": _sb([16 * 8, 10], F16), "pout": _sb([16 * 8, 10], F16), "sl": _sb([16, 10], F16), "roff": _sb([128 * 8], U16), "rf": _sb([128 * 8], F32),
+    "ai": _sb([144], I32), "ip": _sb([4], I32), "pm": _sb([8], I32), "col": _sb([8], F32), "ti": _sb([144], I32), "lab0": _sb([128], BF),
+    "za": _sb([144], BF), "zm": _sb([144], BF), "zu": _sb([144], BF), "idb": _sb([128], BF), "idn": _sb([128], BF), "idh": _sb([128], BF),
+    "id8": _sb([128], BF), "id8n": _sb([128], BF), "idq": _sb([128], BF), "idqn": _sb([128], BF),
+    "f1": _sb([128], F16), "f1n": _sb([128], F16), "fh": _sb([128], F16), "fhn": _sb([128], F16), "bones": _sb([128], F32),
+    "off": _sb([144], BF), "c2": _sb([128], BF), "cq": _sb([128], BF), "cu": _sb([8], BF), "c1": _sb([128], BF), "low": _sb([128], F32),
+    "bc128": _sb([8], U16), "bc64": _sb([8], U16), "bc8": _sb([8], U16), "tl": _sb([8], U16), "negi": _sb([8], F32), "mm8": _sb([64], F32),
     "pk": _sb([128], F32), "dup": _sb([16, 16], F32), "tr": _sb([256], F32), "wi": _sb([128], I32), "hi3": _sb([16, 8], I32), "lo3": _sb([16, 8], I32),
-    "s1": _sb([128], F32), "szb": _sb([128], F32), "wp": _sb([64], I32), "bb": _sb([64], I32), "ee": _sb([64], I32),
-    "poff": _sb([64], U16), "val": _sb([64], F32), "sy": _sb([64], F32), "yoff": _sb([8], U16), "y": _sb([128], BF),
-    "wr": _sb([128], I32), "q4": _sb([128], I32), "flag": _sb([128], BF), "ls": _sb([128], I32), "lm": _sb([128], I32),
-    "ui": _sb([8], I32), "ua": _sb([8], I32), "uf": _sb([8], F32), "uoff": _sb([8], U16), "item": _sb([128], BF), "ub": _sb([64], F32),
-    "rlow": _sb([8, 16], F32), "prod": _sb([64], I32), "sh": _sb([64], I32), "sm": _sb([64], I32), "nw": _sb([64], I32),
-    "phigh": _sb([64], F32), "d1": _sb([64], F32), "d2": _sb([64], F32), "m1": _sb([64], F32),
-    "cnt": _sb([4], F32), "acv": _sb([4], I32), "a31": _sb([4], I32), "thr": _sb([4], F32), "th1": _sb([4], F32),
-    "sx": _sb([64], I32), "bits": _sb([192], I32), "rn": _sb([128], F32), "xa": _sb([16, 16], F32), "xb": _sb([16, 16], F32),
+    "s1": _sb([136], F32), "keep": _sb([128], BF), "wp": _sb([64], I32), "bb": _sb([64], I32), "t8": _sb([8], F32), "h": _sb([128], BF),
+    "thrb": _sb([128], F32), "poff": _sb([64], U16), "sy": _sb([128], F32), "yoff": _sb([8], U16), "y": _sb([128], BF),
+    "wr": _sb([128], I32), "q4": _sb([128], I32), "flag": _sb([128], BF), "far": _sb([128], BF), "n16": _sb([128], BF),
+    "qi": _sb([8], I32), "fr": _sb([8], F32), "uoff": _sb([8], U16), "item": _sb([128], BF),
+    "prod": _sb([64], I32), "sh": _sb([64], I32), "sm": _sb([64], I32), "nw": _sb([64], I32),
+    "pl_": _sb([64], F32), "ph": _sb([64], F32), "plu": _sb([64], F32), "phu": _sb([64], F32), "pa": _sb([64], F32),
+    "d1": _sb([64], F32), "d2": _sb([64], F32), "lf": _sb([64], F32), "junk": _sb([64], F32),
+    "cnt": _sb([4], F32), "af": _sb([4], F32), "qb": _sb([8], BF), "xx": _sb([4], F32), "thr": _sb([4], F32), "th2": _sb([4], F32),
+    "sx": _sb([64], I32), "bits": _sb([192], I32), "xa": _sb([16, 16], F32), "xb": _sb([16, 16], F32),
     "op": _sb([128], F32), "orr": _sb([128], F32),
     "pK": ("psum", [128, 512], F32), "pA": ("psum", [128, 32, 16], F32), "pB": ("psum", [128, 32, 16], F32), "pS": ("psum", [128, 512], F32),
-    "pY": ("psum", [128, 512], F32), "pD": ("psum", [128, 512], F32), "pF": ("psum", [128, 512], F32), "pV": ("psum", [128, 512], F32),
+    "pC": ("psum", [128, 32, 16], F32), "pD": ("psum", [128, 32, 16], F32), "pX": ("psum", [128, 512], F32), "pV": ("psum", [128, 512], F32),
 }
 NDMA = 12
 SEMAPHORES = (["cV", "cS", "cP", "cG", "sent"] + ["dm%d" % k for k in range(NDMA)]
-              + ["%s%d" % (n, s) for n in ("az", "al", "ap", "ar") for s in range(1, ST)])
+              + ["%s%d" % (n, s) for n in ("az", "al", "ap", "ar") for s in range(1, 8)])
+BIGH = 2.0 ** 23
 
 
 def rank_program(g, core, T, topo):
@@ -51,6 +58,7 @@ def rank_program(g, core, T, topo):
     writer, readers, banks = {}, {}, {}
     clock = {q: {} for q in queue}
     ndma = [0]
+    name = [""]
 
     def need(q, dep, waits):
         if isinstance(dep, tuple):
@@ -75,8 +83,7 @@ def rank_program(g, core, T, topo):
     def op(q, fn, r=(), w=(), kind="c"):
         deps = []
         for k in r:
-            if k in writer:
-                deps.append(writer[k])
+            deps.append(writer[k])
         for k in w:
             if k in writer:
                 deps.append(writer[k])
@@ -94,7 +101,7 @@ def rank_program(g, core, T, topo):
         if kind == "dma":
             tok = ("dm%d" % ndma[0], 16)
             ndma[0] += 1
-        ops.append({"q": q, "fn": fn, "waits": waits, "kind": kind, "used": False, "clock": dict(clock[q]), "tok": tok})
+        ops.append({"q": q, "fn": fn, "waits": waits, "kind": kind, "used": False, "clock": dict(clock[q]), "tok": tok, "name": name[0], "r": r, "w": w})
         if kind != "send":
             for k in r:
                 readers.setdefault(k, []).append(tok)
@@ -117,29 +124,37 @@ def rank_program(g, core, T, topo):
     def cp(out, a, r, w):
         op("V", lambda: g.vector.tensor_copy(out, a), r, w)
 
-    def scan(out, d0, d1, o0, o1, r, w):
-        op("V", lambda: g.vector.tensor_tensor_scan(out, d0, d1, 0.0, o0, o1), r, w)
+    def scan(out, d0, d1, init, o0, o1, r, w):
+        op("V", lambda: g.vector.tensor_tensor_scan(out, d0, d1, init, o0, o1), r, w)
 
     def ms(ap, c, w):
         op("V", lambda: g.vector.memset(ap, c), (), w)
 
     def mm(out, l, rh, st, sp, r, w):
+        if st and w[0].startswith("pS:"):
+            w = w + ["open"]
         op("P", lambda: g.tensor.matmul(out, l, rh, st, sp), r, w)
 
-    def act(out, a, f, r, w, scale=1.0):
-        op("S", lambda: g.scalar.activation(out, a, f, scale=scale), r, w)
+    def act(out, a, f, r, w, scale=1.0, bias=0.0):
+        op("S", lambda: g.scalar.activation(out, a, f, bias=bias, scale=scale), r, w)
 
     def dma(q, out, a, r, w):
         return op(q, lambda: queue[q].dma_start(out, a), r, w, kind="dma")
 
     sent = [0]
 
-    def send(dst_rank, out, a, sem, r):
+    def send(dst_rank, pairs, sem, r):
         dst = T.cores[dst_rank]
         rid, pid, _ = topo.addr(dst)
-        m = topo.mask(core, dst)
-        sent[0] += len(topo.engines(core, dst))
-        op("G", lambda: g.remote_dma(out, a, T.sem[sem], T.sem.sent, pid, rid, m), r, (), kind="send")
+        eng = topo.engines(core, dst)
+        sent[0] += len(eng)
+        if len(pairs) == 1:
+            op("G", lambda: g.remote_dma(pairs[0][0], pairs[0][1], T.sem[sem], T.sem.sent, pid, rid, topo.mask(core, dst)), r, (), kind="send")
+            return
+        n = len(eng) // len(pairs)
+        trs = [RemoteDMATransfer(dst_ids=[DstId(rid=rid, pnc=pid)], dma_engine_mask=sum(1 << e for e in eng[n * k:n * k + n]),
+                                 remote_sem=T.sem[sem], src=a, dst=out) for k, (out, a) in enumerate(pairs)]
+        op("G", lambda: g.remote_dma_fused(trs, local_sem=T.sem.sent), r, (), kind="send")
 
     def lands(src_rank, calls):
         return calls * len(topo.engines(T.cores[src_rank], core))
@@ -147,43 +162,51 @@ def rank_program(g, core, T, topo):
     def blk(t, s, n, a=0, b=None):
         return t[:, n * s + a:n * s + (n if b is None else b)]
 
+    def zin(s, a=0, b=8):
+        return T.a[:, 16 * (AW * s + 128 + a):16 * (AW * s + 128 + b)]
+
+    def pv(t, s, h, k):
+        return t[:, 16 * s + 8 * h:16 * s + 8 * h + 8, k:k + 8]
+
     prev, nxt = (rank - HOP) % NR, (rank + HOP) % NR
     for s in range(1, ST):
         writer["z%d" % s] = ("az%d" % s, lands(prev, 1))
-        writer["l%d" % s] = ("al%d" % s, lands(prev, 1))
+        writer["l%d" % s] = writer["j%d" % s] = ("al%d" % s, lands(prev, 1))
         writer["p%d" % s] = ("ap%d" % s, lands(prev, 1))
         writer["ro%d" % s] = writer["rf%d" % s] = ("ar%d" % s, lands((rank - HOP * s) % NR, 2))
 
     dma("Y", T.pri[:], T.pr[:], (), ["pri"])
-    dma("Y", T.pli[:], T.pl[:], (), ["pli"])
-    dma("S", T.tab[:], T.xt[:], (), ["tab"])
-    dma("Y", blk(T.zin, 0, 128), T.z0[:], (), ["z0"])
-    dma("Y", T.thi[:, 0:1], T.th[:], (), ["thi"])
+    dma("S", T.pli[:], T.pl[:], (), ["pli"])
+    dma("Y", T.tab[:], T.xt[:], (), ["tab"])
+    dma("S", T.thi[:, 0:1], T.th[:], (), ["thi"])
+    dma("S", zin(0), T.z0[:], (), ["z0"])
 
     op("G", lambda: g.iota(T.ip[:, 0:1], [[0, 1]], 0, 1), (), ["ip"])
     op("G", lambda: g.iota(T.ai[:], [[1, 144]], 0, 0), (), ["ai"])
-    op("G", lambda: g.iota(T.lab0[:], [[0, 8], [1, 8], [8, 2]], 0, 0, allow_small_or_imprecise_dtypes=True), (), ["lab0"])
-    BIG = 1.0e29
-    for t, c in (("c8", -8192.0), ("cq", -0.25), ("c0", 0.0), ("c4", 4096.0)):
+    op("G", lambda: g.iota(T.lab0[:], [[0, 8], [1, 8], [8, 2]], -2, 0, allow_small_or_imprecise_dtypes=True), (), ["lab0"])
+    op("G", lambda: g.iota(T.sx[:], [[0, 8], [1, 8]], 7, 0), (), ["sx"])
+    op("G", lambda: g.iota(T.ti[:, 128:144], [[-1, 8], [0, 2]], 0, 0), (), ["tib"])
+    for t, c in (("c2", -2.0), ("cq", -0.25), ("cu", -15.5 / 32), ("c1", -1.0), ("low", -1.0e9), ("junk", 0.0), ("pk", 0.0)):
         ms(T[t][:], c, [t])
-    masks = (("rs16", 16, -BIG, BIG), ("rs8", 8, -BIG, BIG), ("kp16", 16, 0.0, 1.0), ("kp8", 8, 0.0, 1.0))
-    for t, n, lo, hi in masks:
-        ms(T[t][:], hi, [t])
-    for t, n, lo, hi in masks:
-        ms(T[t][:, 0::n], lo, [t])
-    ms(T.a31[:, 0:1], 0, ["a31"])
+    ms(T.s1[:, 0:8], -1.0e9, ["s1"])
+    ms(T.af[:, 0:1], 2048.0, ["af"])
     for k, m in enumerate((31, 112, 8, 15)):
         ts(T.pm[:, k:k + 1], T.ip[:, 0:1], m, None, A.bitwise_and, None, ["ip"], ["pm%d" % k])
     cp(T.col[:, 0:1], T.pm[:, 0:1], ["pm0"], ["col0"])
     cp(T.col[:, 1:2], T.pm[:, 1:2], ["pm1"], ["col1"])
     ts(T.col[:, 2:3], T.pm[:, 1:2], 15.0, None, A.add, None, ["pm1"], ["col2"])
-    ts(T.col[:, 3:4], T.pm[:, 2:3], 2.0, 15.0, A.mult, A.add, ["pm2"], ["col3"])
-    ts(T.col[:, 4:5], T.pm[:, 3:4], 32.0, None, A.mult, None, ["pm3"], ["col4"])
+    ts(T.col[:, 3:4], T.pm[:, 2:3], 2.0, 16.0, A.mult, A.add, ["pm2"], ["col3"])
+    cp(T.col[:, 4:5], T.pm[:, 3:4], ["pm3"], ["col4"])
     cp(T.col[:, 5:6], T.ip[:, 0:1], ["ip"], ["col5"])
     ts(T.tl[:], T.ai[:, 0:8], 32.0, T.col[:, 0:1], A.mult, A.add, ["ai", "col0"], ["tl"])
     ts(T.idb[:], T.ai[:, 0:128], T.col[:, 5:6], None, A.is_equal, None, ["ai", "col5"], ["idb"])
-    ts(T.za[:], T.ai[:], T.col[:, 2:3], 65536.0, A.is_equal, A.mult, ["ai", "col2"], ["za"])
-    ts(T.zm[:], T.ai[:], T.col[:, 2:3], -131072.0, A.is_equal, A.mult, ["ai", "col2"], ["zm"])
+    for t, wgt in (("za", 16.0), ("zm", -32.0), ("zu", 1.0 / 32)):
+        ts(T[t][:], T.ai[:], T.col[:, 2:3], wgt, A.is_equal, A.mult, ["ai", "col2"], [t])
+    ts(T.ti[:, 0:128], T.ai[:, 0:128], 4, None, A.arith_shift_right, None, ["ai"], ["ti"])
+    cp(T.pout[:, :, 9], T.pk[:], ["pk"], ["pz"])
+    cp(T.pin[:, 0:16, 9], T.junk[:, 0:16], ["junk"], ["p0z"])
+    cp(T.sl[:, :, 8], T.junk[:, 0:16], ["junk"], ["slz"])
+    ts(T.off[:], T.ti[:], 2.0 ** 18, None, A.mult, None, ["ti", "tib"], ["off"])
 
     ts(T.pk[:], T.pli[:], 4096.0, None, A.mult, None, ["pli"], ["pk"])
     for e in range(2):
@@ -195,252 +218,297 @@ def rank_program(g, core, T, topo):
     for h in range(2):
         cp(T.roff[:, 64 * h:64 * h + 64], T.lo3[:, h::2, :], ["lo3"], ["ro0h%d" % h])
     cp(T.rf[:, 0:64], T.lo3[:, 0::2, :], ["lo3"], ["rf0a"])
-    tt(T.rf[:, 64:128], T.lo3[:, 1::2, :], T.lo3[:, 0::2, :], A.subtract, ["lo3"], ["rf0"])
+    tt(T.d1[:], T.lo3[:, 1::2, :], T.lo3[:, 0::2, :], A.subtract, ["lo3"], ["d1"])
     for h in range(2):
-        cp(T.pin[:, 64 * h:64 * h + 64], T.hi3[:, h::2, :], ["hi3"], ["p0" if h else "p0a"])
+        ts(pv(T.pin, 0, h, 1), T.hi3[:, h::2, :], -2048.0, None, A.add, None, ["hi3"], ["p0a%d" % h])
+        ts(T.pin[:, 8 * h:8 * h + 8, 0], T.hi3[:, h::2, 7], -2048.0, None, A.add, None, ["hi3", "p0z"], ["p0b%d" % h])
+    ts(T.rf[:, 64:128], T.d1[:], 1.0 / BIGH, None, A.mult, None, ["d1"], ["rf0"])
     writer["ro0"] = writer["ro0h1"]
+    writer["p0"] = writer["p0b1"]
 
-    for t, wgt in (("idn", -1.0), ("idf", 1.0), ("idnf", -1.0), ("idh", 0.5), ("id8", 32768.0)):
+    for t, wgt in (("idn", -1.0), ("idh", 0.5), ("id8", 8.0), ("id8n", -8.0), ("idq", 0.125), ("idqn", -0.125),
+                   ("f1", 1.0), ("f1n", -1.0), ("fh", 0.5), ("fhn", -0.5)):
         ts(T[t][:], T.ai[:, 0:128], T.col[:, 5:6], wgt, A.is_equal, A.mult, ["ai", "col5"], [t])
-    ts(T.bc128[:], T.ai[:, 0:8], 16.0, 15.0, A.mult, A.add, ["ai"], ["bc128"])
+    ts(T.bc128[:], T.ai[:, 0:8], 16.0, 16.0, A.mult, A.add, ["ai"], ["bc128"])
     ts(T.bc64[:], T.ai[:, 0:8], 32.0, T.col[:, 3:4], A.mult, A.add, ["ai", "col3"], ["bc64"])
-    ts(T.base[:], T.ai[:, 0:8], 512.0, T.col[:, 4:5], A.mult, A.add, ["ai", "col4"], ["base"])
-    ts(T.ti[:], T.ai[:, 0:128], 112, None, A.bitwise_and, None, ["ai"], ["ti"])
-    ts(T.sx[:], T.ai[:, 0:64], 7, None, A.bitwise_and, None, ["ai"], ["sx"])
-    ts(T.bones[:], T.ti[:], T.col[:, 1:2], None, A.is_equal, None, ["ti", "col1"], ["bones"])
-    ts(T.lin[:, 0:128], T.lab0[:], 4096.0, None, A.mult, None, ["lab0"], ["l0a"])
-    ts(T.lin[:, 128:192], T.sx[:], 2.0, 4096.0, A.add, A.mult, ["sx"], ["l0"])
-    ts(T.th1[:, 0:1], T.thi[:, 0:1], 1.125, None, A.add, None, ["thi"], ["th1"])
-    ts(T.mm8[:], T.sx[:], 8.0, 4096.0, A.add, A.mult, ["sx"], ["mm8"])
+    cp(T.bc8[:], T.ai[:, 0:8], ["ai"], ["bc8"])
+    ts(T.negi[:], T.ai[:, 0:8], -16.0, T.col[:, 4:5], A.mult, A.subtract, ["ai", "col4"], ["negi"])
+    ts(T.wi[:], T.ai[:, 0:128], 112, None, A.bitwise_and, None, ["ai"], ["wi"])
+    ts(T.jin[:, 0:64], T.sx[:], 7, None, A.bitwise_and, None, ["sx"], ["j0"])
+    cp(T.lin[:, 0:128], T.lab0[:], ["lab0"], ["l0"])
+    ts(T.thr[:, 0:1], T.thi[:, 0:1], 1.0, -16.0, A.add, A.mult, ["thi"], ["thr"])
+    ts(T.th2[:, 0:1], T.thi[:, 0:1], 1.0 + 32 * 192, -16.0, A.add, A.mult, ["thi"], ["th2"])
+    ts(T.bones[:], T.wi[:], T.col[:, 1:2], None, A.is_equal, None, ["wi", "col1"], ["bones"])
+    ts(T.mm8[:], T.sx[:], 16.0, None, A.add, None, ["sx"], ["mm8"])
 
     def sel(t, r):
         return t[:, 15 - r:143 - r]
 
-    K, SZ, U, AP_ = T.pK[:, 0:128], T.pS[:, 0:128], T.pS[:, 128:192], T.pS[:, 192:193]
-    R8, HF, Dp, DP, Fp = T.pF[:, 128:256], T.pY[:, 128:256], T.pD[:, 0:128], T.pD[:, 128:192], T.pF[:, 0:64]
-    tP, PL, C7, bR, tR, LF, PA = (T.pV[:, 0:64], T.pV[:, 64:128], T.pV[:, 128:256], T.pV[:, 256:320], T.pV[:, 320:384],
-                                  T.pV[:, 384:448], T.pV[:, 448:512])
+    K, SZ = T.pK[:, 0:128], T.pK[:, 129:144:2]
+    Dp, HF, Fp, AP_, DL = T.pS[:, 0:128], T.pS[:, 128:256], T.pS[:, 256:320], T.pS[:, 320:321], T.pS[:, 384:512]
+    U, R8, DP, SG = T.pX[:, 0:8], T.pX[:, 128:256], T.pX[:, 256:320], T.pX[:, 320:384]
+    tP, tR, D1, D2, M1, M2 = (T.pV[:, 64 * k:64 * k + 64] for k in range(6))
+    HH = T.pV[:, 384:512]
     tiles = ((T.pA, "pA:t"), (T.pB, "pB:t"))
+    ftiles = ((T.pC, "pC:t"), (T.pD, "pD:t"))
     win = T.tab[:, :]
     outs = []
 
-    def tile(hh, src, key):
-        for m in range(8):
-            mm(tiles[hh][0][:, m::8, :], T.idb[:], src, True, True, ["idb", key], [tiles[hh][1]])
-
     def send_r(s):
         d = (rank + HOP * s) % NR
-        send(d, blk(T.roff, s, 128), blk(T.roff, 0, 128), "ar%d" % s, ["ro0h0", "ro0h1"])
-        send(d, blk(T.rf, s, 128), blk(T.rf, 0, 128), "ar%d" % s, ["rf0a", "rf0"])
+        send(d, [(blk(T.roff, s, 128), blk(T.roff, 0, 128))], "ar%d" % s, ["ro0h0", "ro0h1"])
+        send(d, [(blk(T.rf, s, 128), blk(T.rf, 0, 128))], "ar%d" % s, ["rf0a", "rf0"])
 
-    def gather_r(s):
-        for k, (lo_, hi_) in enumerate(CH):
-            src = win.indirect(blk(T.roff, s, 128, lo_ // 16, hi_ // 16))
-            if s == 0 and k >= 3:
-                cp(T.a[:, lo_:hi_], src, ["tab", "ro%d" % s], ["a%d" % k])
+    def near_calls(s):
+        zk, lk, pk_, c0 = "z%d" % s, "l%d" % s, "p%d" % s, AW * s
+
+        def parts(lo_, hi_):
+            return ["a%d" % k for k, c in enumerate(CH) if c[1] < hi_ and c[2] > lo_]
+
+        def gather(k):
+            q, lo_, hi_ = CH[k]
+            src = win.indirect(blk(T.roff, s, 128, lo_, hi_))
+            if q == "V" or (s == 0 and k == 4):
+                cp(T.a[:, 16 * (c0 + lo_):16 * (c0 + hi_)], src, ["tab", "ro%d" % s], ["a%d" % k])
             else:
-                act(T.a[:, lo_:hi_], src, ACT.Copy, ["tab", "ro%d" % s], ["a%d" % k])
+                act(T.a[:, 16 * (c0 + lo_):16 * (c0 + hi_)], src, ACT.Copy, ["tab", "ro%d" % s], ["a%d" % k])
 
-    def ztiles(s):
-        for hh in range(2):
-            if hh == 0:
-                mm(K, T.idb[:], T.c8[:], True, False, ["idb", "c8"], ["pK:k"])
-            tile(hh, blk(T.zin, s, 128, 64 * hh, 64 * hh + 64), "z%d" % s)
+        def init():
+            mm(T.pK[:, 0:144], T.idb[:], T.off[:], True, False, ["idb", "off"], ["pK:k"])
+            mm(K, T.idb[:], T.c2[:], False, False, ["c2"], ["pK:k"])
 
-    def nearest(s):
-        for r in range(16):
-            mm(T.pK[:, 0:128:2], sel(T.za, r), T.a[:, r:1024:16], False, False, ["a0", "a1"], ["pK:k"])
-
-        for k in ((3, 4, 0, 1, 2) if s == 0 else range(5)):
-            lo_, hi_ = CH[k]
-            t = tiles[lo_ // 512 % 2]
-            tt(T.mx[:, lo_:hi_], T.a[:, lo_:hi_], t[0][:, lo_ % 512 // 16:(hi_ - 1) % 512 // 16 + 1, :], A.max, ["a%d" % k, t[1]], ["mx%d" % k])
-        for r in range(16):
-            mm(T.pK[:, 0:128:2], sel(T.zm, r), T.mx[:, r:1024:16], False, False, ["zm", "mx0", "mx1"], ["pK:k"])
-        mm(K, T.idn[:], blk(T.lin, s, 192, 0, 128), False, False, ["idn", "l%d" % s], ["pK:k"])
-        for r in range(16):
-            mm(T.pK[:, 1:128:2], sel(T.za, r), T.a[:, 1024 + r:2048:16], False, False, ["a2", "a3", "a4"], ["pK:k"])
-        for r in range(16):
-            mm(T.pK[:, 1:128:2], sel(T.zm, r), T.mx[:, 1024 + r:2048:16], False, r == 15, ["mx2", "mx3", "mx4"], ["pK:k"])
-        if s:
-            cp(T.acv[:, 0:1], AP_, ["pS:a"], ["acv"])
-            ts(T.a31[:, 0:1], T.acv[:, 0:1], 31, None, A.bitwise_and, None, ["acv"], ["a31"])
-        ts(T.thr[:, 0:1], T.a31[:, 0:1], T.th1[:, 0:1], -65536.0, A.add, A.mult, ["a31", "th1"], ["thr"])
-        mm(SZ, T.idb[:], T.c0[:], True, False, ["c0"], ["pS:sz"])
-        for r in range(16):
-            mm(T.pS[:, 0:128:16], sel(T.za, r), T.zin[:, 128 * s + r:128 * s + 128:16], False, r == 15, ["za"], ["pS:sz"])
-        mm(DP, T.idf[:], blk(T.pin, s, 128, 64, 128), True, False, ["idf", "p%d" % s], ["pD:dp"])
-        mm(DP, T.idnf[:], blk(T.pin, s, 128, 0, 64), False, True, ["idnf", "p%d" % s], ["pD:dp"])
-
-
-    def step(s):
-        last = s == ST - 1
-        z, zk, lk, pk_, rk = blk(T.zin, s, 128), "z%d" % s, "l%d" % s, "p%d" % s, "rf%d" % s
-        plo, phi = blk(T.pin, s, 128, 0, 64), blk(T.pin, s, 128, 64, 128)
-        rlo, dr = blk(T.rf, s, 128, 0, 64), blk(T.rf, s, 128, 64, 128)
-        k = (s + 1) % 8
-
-        def poff():
-            cp(T.poff[:], PL, ["pV:pl"], ["poff"])
-            act(T.v[:, 0:512], win.indirect(T.poff[:, 0:32]), ACT.Copy, ["tab", "poff"], ["v0"])
-
-        def flag():
-            tt(T.flag[:], T.q4[:], C7, A.is_lt, ["q4", "pV:c7"], ["flag"])
-            mm(R8, T.idb[:], T.c4[:], True, False, ["c4"], ["pF:r8"])
-            mm(R8, T.id8[:], T.flag[:], False, False, ["id8", "flag"], ["pF:r8"])
-            mm(T.pF[:, 128:256:2], T.id8[:], T.flag[:, 1::2], False, False, ["flag"], ["pF:r8"])
-            mm(T.pF[:, 129:256:2], T.id8[:], T.flag[:, 0::2], False, True, ["flag"], ["pF:r8"])
-
-        def y():
-            cp(T.y[:], win.indirect(T.yoff[:, 0:8]), ["tab", "yoff"], ["y"])
-            mm(Dp, T.idb[:], T.y[:], True, False, ["y"], ["pD:d"])
-            mm(Dp, T.idn[:], z, False, True, [zk], ["pD:d"])
-            act(blk(T.zout, s, 128), Dp, ACT.Abs, ["pD:d"], ["zo%d" % s])
-            if last:
-                outs.append(dma("Y", T.yz[:], blk(T.zout, s, 128), ["zo%d" % s], ()))
-            else:
-                send(nxt, blk(T.zin, s + 1, 128), blk(T.zout, s, 128), "az%d" % (s + 1), ["zo%d" % s])
-            act(T.v[:, 512:1024], win.indirect(T.poff[:, 32:64]), ACT.Copy, ["tab", "poff"], ["v1"])
-            mm(U, T.idb[:], T.c0[:, 0:64], True, False, [], ["pS:u"])
-            for r in range(16):
-                mm(T.pS[:, 128:192:8], sel(T.za, r), T.y[:, r::16], False, r == 15, ["y"], ["pS:u"])
-            mm(HF, T.idh[:], T.y[:], True, False, ["idh", "y"], ["pY:h"])
-            mm(HF, T.idh[:], z, False, False, [zk], ["pY:h"])
-            mm(HF, T.idb[:], T.cq[:], False, True, ["cq"], ["pY:h"])
-            mm(T.pA[:], T.idb[:], T.v[:, 0:512], True, False, ["v0"], ["pA:t"])
+        def ztile(hh):
             for m in range(8):
-                mm(T.pA[:, m::8, :], T.idn[:], T.y[:, 0:64], False, m == 7, ["y"], ["pA:t"])
-            act(T.mf[:, 0:512], T.pA[:], ACT.Abs, ["pA:t"], ["mf0"], 0.5)
-            tile(1, T.y[:, 64:128], "y")
+                mm(tiles[hh][0][:, m::8, :], T.idb[:], zin(s, 4 * hh, 4 * hh + 4), True, True, ["idb", zk], [tiles[hh][1]])
 
-        def rlow():
-            tt(T.rlow[:, :, 0:8], rlo, tR, A.add, [rk, "pV:tr"], ["rlowa"])
-            if k:
-                tt(T.rlow[:, :, 8:16], rlo, tR, A.add, [rk, "pV:tr"], ["rlowb"])
+        def big(k):
+            lo_, hi_, r0, n = MX[k]
+            t = tiles[lo_ // 32 % 2]
+            tt(T.mx[:, lo_:hi_, r0::n], T.a[:, 16 * (c0 + lo_) + r0:16 * (c0 + hi_):n], t[0][:, lo_ % 32:(hi_ - 1) % 32 + 1, r0::n], A.max,
+               parts(lo_, hi_) + [t[1]], ["mx%d" % k])
 
-        def ub():
-            scan(T.ub[:, 32:64], T.kp8[:, 32:64], T.pS[:, 160:192], A.mult, A.add, ["kp8", "pS:u"], ["ub"])
-            mm(Fp, T.idb[:], T.c8[:, 0:64], True, False, [], ["pF:f"])
-            mm(T.pF[:, 32:64], T.idf[:], T.ub[:, 32:64], False, False, ["ub"], ["pF:f"])
+        def sum_a(h):
             for r in range(16):
-                mm(T.pF[:, 32:64], sel(T.za, r), T.v[:, 512 + r:1024:16], False, False, ["v1"], ["pF:f"])
+                mm(T.pK[:, h:128 + 16 * h:2], sel(T.za, r), T.a[:, 16 * (c0 + 64 * h) + r:16 * (c0 + 64 + 72 * h):16], False, False,
+                   parts(64 * h, 64 * h + 64) + [zk if h else "za"], ["pK:k"])
 
-        def lo():
-            ts(blk(T.lout, s, 192, 0, 128), T.lm[:], 0.0, None, A.add, None, ["lm"], ["lo%d" % s])
-            send(nxt, blk(T.lin, s + 1, 192), blk(T.lout, s, 192), "al%d" % (s + 1), ["loa%d" % s, "lo%d" % s])
+        def sum_m(h, r0, n):
+            r_ = ["mx%d" % k for k, c in enumerate(MX) if c[0] // 64 == h and (c[3] == 1 or n == 1 or c[2] == r0)]
+            for r in range(r0, 16, n):
+                mm(T.pK[:, h:128:2], sel(T.zm, r), T.mx[:, 64 * h:64 * h + 64, r], False, h == 1 and r == 15, r_ + ["zm"], ["pK:k"])
+
+        def dp():
+            mm(DP, T.f1[:], pv(T.pin, s, 1, 0), True, False, ["f1", pk_], ["pX:dp"])
+            mm(DP, T.f1n[:], pv(T.pin, s, 0, 0), False, True, ["f1n", pk_], ["pX:dp"])
+
+        def sg():
+            mm(SG, T.idq[:], T.lin[:, 128 * s + 1:128 * s + 128:2], True, False, ["idq", lk], ["pX:sg"])
+            mm(SG, T.idqn[:], T.lin[:, 128 * s:128 * s + 128:2], False, True, ["idqn", lk], ["pX:sg"])
+
+        def sl():
+            for h in range(2):
+                tt(pv(T.sl, 0, h, 0), pv(T.pin, s, h, 1), SG, A.mult, [pk_, "pX:sg", "slz"], ["sl%d" % h])
+
+        def dl():
+            b, a_ = T.pS[:, 385:512:2], T.pS[:, 384:512:2]
+            terms = [(T.fh, T.pin, s, 0, 1), (T.fh, T.pin, s, 1, 1), (T.fhn, T.pin, s, 0, 2), (T.fhn, T.pin, s, 1, 2),
+                     (T.fhn, T.sl, 0, 0, 0), (T.fhn, T.sl, 0, 0, 1), (T.fh, T.sl, 0, 1, 0), (T.fh, T.sl, 0, 1, 1)]
+            for k, (w_, t, s_, h, k0) in enumerate(terms):
+                mm(b, w_[:], pv(t, s_, h, k0), k == 0, False, ["fh", "fhn", pk_ if k < 4 else "sl%d" % h], ["pS:dl"])
+            mm(a_, T.f1[:], pv(T.sl, 0, 0, 0), False, False, ["f1", "sl0"], ["pS:dl"])
+            mm(a_, T.f1n[:], pv(T.sl, 0, 1, 0), False, True, ["f1n", "sl1"], ["pS:dl"])
+
+        call = {
+            "init": init, "dp": dp, "sg": sg, "sl": sl, "dl": dl,
+            "lab": lambda: mm(K, T.idn[:], blk(T.lin, s, 128), False, False, ["idn", lk], ["pK:k"]),
+            "sm0": lambda: sum_m(0, 0, 1), "sm1": lambda: sum_m(1, 0, 2), "sm2": lambda: sum_m(1, 1, 2),
+            "af": lambda: act(T.af[:, 0:1], AP_, ACT.Identity, ["pS:a"], ["af"], bias=2048.0),
+            "qb": lambda: act(T.qb[:, 0:1], AP_, ACT.Identity, ["pS:a"], ["qb"], 1.0 / 32, 192 - 15.5 / 32),
+            "xx": lambda: act(T.xx[:, 0:1], AP_, ACT.Identity, ["pS:a", "th2"], ["xx"], -16.0, T.th2[:, 0:1]),
+            "thr": lambda: act(T.thr[:, 0:1], T.qb[:, 0:1], ACT.Identity, ["qb", "xx"], ["thr"], 512.0, T.xx[:, 0:1]),
+        }
+        for k in range(len(CH)):
+            call["g%d" % k] = lambda k=k: gather(k)
+        for k in range(len(MX)):
+            call["x%d" % k] = lambda k=k: big(k)
+        for h in range(2):
+            call["zt%d" % h] = lambda h=h: ztile(h)
+            call["sa%d" % h] = lambda h=h: sum_a(h)
+        return call
+
+    def step_calls(s):
+        last = s == ST - 1
+        z, zk, lk, jk, pk_, rk = zin(s), "z%d" % s, "l%d" % s, "j%d" % s, "p%d" % s, "rf%d" % s
+        rlo, dr = blk(T.rf, s, 128, 0, 64), blk(T.rf, s, 128, 64, 128)
+        zo = blk(T.zout, s, 128)
+
+        def r8():
+            mm(R8, T.idb[:], T.c1[:], True, False, ["c1"], ["pX:r8"])
+            mm(R8, T.idb[:], T.n16[:], False, False, ["n16"], ["pX:r8"])
+            mm(R8, T.id8[:], T.flag[:], False, False, ["id8", "flag"], ["pX:r8"])
+            mm(T.pX[:, 128:256:2], T.id8n[:], T.flag[:, 1::2], False, False, ["id8n", "flag"], ["pX:r8"])
+            mm(T.pX[:, 129:256:2], T.id8n[:], T.flag[:, 0::2], False, True, ["flag"], ["pX:r8"])
+
+        def u():
+            mm(U, T.idb[:], T.cu[:], True, False, ["cu"], ["pX:u"])
+            for r in range(16):
+                mm(U, sel(T.zu, r), T.y[:, r::16], False, r == 15, ["zu", "y"], ["pX:u"])
+
+        def zd():
+            mm(Dp, T.idb[:], T.y[:], True, False, ["y"], ["pS:d"])
+            mm(Dp, T.idn[:], z, False, True, [zk], ["pS:d"])
+
+        def hf():
+            mm(HF, T.idh[:], T.y[:], True, False, ["idh", "y"], ["pS:h"])
+            mm(HF, T.idh[:], z, False, False, [zk], ["pS:h"])
+            mm(HF, T.idb[:], T.cq[:], False, True, ["cq"], ["pS:h"])
+
+        def zsend():
+            if last:
+                outs.append(dma("Y", T.yz[:], zo, ["zo%d" % s], ()))
+            else:
+                send(nxt, [(zin(s + 1), zo)], "az%d" % (s + 1), ["zo%d" % s])
+
+        def fd(hh):
+            t, key = ftiles[hh]
+            for m in range(8):
+                mm(t[:, m::8, :], T.idn[:], T.y[:, 64 * hh:64 * hh + 64], m == 0, False, ["y"], [key])
+            mm(t[:], T.idb[:], T.v[:, 512 * hh:512 * hh + 512], False, True, ["v%d" % hh], [key])
+
+        def fa(k):
+            hh, r0 = k % 2, 8 * (k // 2)
+            act(T.mf[:, 32 * hh:32 * hh + 32, r0:r0 + 8], ftiles[hh][0][:, :, r0:r0 + 8], ACT.Abs, [ftiles[hh][1]], ["mf%d" % k], 0.5)
+
+        def fs(b):
+            for r in range(8 * b, 8 * b + 8):
+                mm(Fp, sel(T.zm, r), T.mf[:, :, r], r == 0, r == 15, ["mf%d" % (2 * b), "mf%d" % (2 * b + 1)], ["pS:f", "open"])
+
+        def lsend():
+            send(nxt, [(blk(T.lin, s + 1, 128), blk(T.lout, s, 128)), (blk(T.jin, s + 1, 64), blk(T.jout, s, 64))],
+                 "al%d" % (s + 1), ["lo%d" % s, "jn%d" % s])
 
         def scat():
             cp(win.indirect(T.uoff[:, 0:8]), T.item[:], ["uoff", "item"], ["tab"])
             if last:
                 outs.append(dma("S", T.yx[0:64, :], T.tab[0:64, :], ["tab"], ()))
                 outs.append(dma("Y", T.yx[64:128, :], T.tab[64:128, :], ["tab"], ()))
-            else:
-                gather_r(s + 1)
-
-        def fmax():
-            tt(T.mf[:, 512:1024], T.v[:, 512:1024], T.pB[:], A.max, ["v1", "pB:t"], ["mf1"])
-            for r in range(16):
-                mm(Fp, sel(T.zm, r), T.mf[:, r::16], False, r == 15, ["mf0", "mf1"], ["pF:f"])
-            if not last:
-                ztiles(s + 1)
 
         def po():
-            tt(blk(T.pout, s, 128, 0, 64), T.m1[:], PL, A.add, ["m1", "pV:pl"], ["poa%d" % s])
-            tt(blk(T.pout, s, 128, 64, 128), T.phigh[:], tR, A.add, ["phigh", "pV:tr"], ["po%d" % s])
+            for h, (x, xk, m, mk) in enumerate(((T.pl_, "pl", 4, "pV:m1"), (T.ph, "ph", 5, "pV:m2"))):
+                tt(pv(T.pout, s, h, 1), x[:], T.pV[:, 64 * m:64 * m + 64], A.add, [xk, mk, "pz"], ["po%d%d" % (h, s)])
+                if not last:
+                    tt(T.pout[:, 16 * s + 8 * h:16 * s + 8 * h + 8, 0], x[:, 7::8], T.pV[:, 64 * m + 7:64 * m + 64:8], A.add, [xk, mk], ["pw%d%d" % (h, s)])
             if not last:
-                send(nxt, blk(T.pin, s + 1, 128), blk(T.pout, s, 128), "ap%d" % (s + 1), ["poa%d" % s, "po%d" % s])
-                if s + 2 < ST:
-                    send_r(s + 2)
+                send(nxt, [(T.pin[:, 16 * s + 16:16 * s + 32, :], T.pout[:, 16 * s:16 * s + 16, :])], "ap%d" % (s + 1),
+                     ["po0%d" % s, "po1%d" % s, "pw0%d" % s, "pw1%d" % s])
 
         def cnt():
-            op("V", lambda: g.vector.tensor_reduce(T.cnt[:, 0:1], LF, AxisListType.X, A.add), ["pV:lf"], ["cnt"])
+            op("S", lambda: g.scalar.activation(T.junk[:], T.lf[:], ACT.Copy, accum_out=T.cnt[:, 0:1]), ["lf"], ["cnt", "junk"])
             mm(AP_, T.bones[:], T.cnt[:, 0:1], True, True, ["bones", "cnt"], ["pS:a"])
 
         call = {
-            "s1": lambda: scan(T.s1[:], T.rs16[:], K, A.min, A.max, ["rs16", "pK:k"], ["s1"]),
-            "wp": lambda: tt(T.wp[:], T.s1[:, :].indirect(T.bc64[:, 0:4]), blk(T.lin, s, 192, 128, 192), A.add, ["s1", "bc64", lk], ["wp"]),
-            "bb": lambda: ts(T.bb[:], T.wp[:], 15, 1, A.arith_shift_right, A.bitwise_and, ["wp"], ["bb"]),
-            "ee": lambda: ts(T.ee[:], T.wp[:], 7 << 12, None, A.bitwise_and, None, ["wp"], ["ee"]),
-            "t": lambda: tt(tP, T.bb[:], DP, A.mult, ["bb", "pD:dp"], ["pV:t"]),
-            "pl": lambda: tt(PL, plo, tP, A.add, [pk_, "pV:t"], ["pV:pl"]),
-            "poff": poff,
-            "val": lambda: tt(T.val[:], PL, T.ee[:], A.subtract, ["pV:pl", "ee"], ["val"]),
-            "sy": lambda: scan(T.sy[:], T.rs8[:], T.val[:], A.min, A.max, ["rs8", "val"], ["sy"]),
-            "yoff": lambda: cp(T.yoff[:], T.sy[:, 7::8], ["sy"], ["yoff"]),
-            "y": y,
-            "szb": lambda: scan(T.szb[:], T.kp16[:], SZ, A.mult, A.add, ["kp16", "pS:sz"], ["szb"]),
-            "kd": lambda: tt(C7, K, T.szb[:], A.add, ["pK:k", "szb"], ["pV:c7"]),
-            "c7": lambda: ts(C7, C7, T.thr[:, 0:1], 7.0 * 4096, A.is_le, A.mult, ["pV:c7", "thr"], ["pV:c7"]),
-            "wr": lambda: tt(T.wr[:], T.s1[:, :].indirect(T.bc128[:, 0:8]), blk(T.lin, s, 192, 0, 128), A.add, ["s1", "bc128", lk], ["wr"]),
-            "q4": lambda: ts(T.q4[:], T.wr[:], 15 << 12, None, A.bitwise_and, None, ["wr"], ["q4"]),
-            "flag": flag,
-            "ls": lambda: tt(T.ls[:], T.q4[:], R8, A.add, ["q4", "pF:r8"], ["ls"]),
-            "loa": lambda: ts(blk(T.lout, s, 192, 128, 192), T.ee[:], 8192.0, None, A.add, None, ["ee"], ["loa%d" % s]),
-            "lm": lambda: ts(T.lm[:], T.ls[:], 15 << 12, None, A.bitwise_and, None, ["ls"], ["lm"]),
-            "lo": lo,
-            "ui": lambda: cp(T.ui[:], T.pS[:, 128:192:8], ["pS:u"], ["ui"]),
-            "ua": lambda: ts(T.ua[:], T.ui[:], 16, 31, A.arith_shift_right, A.bitwise_and, ["ui"], ["ua"]),
-            "uf": lambda: tt(T.uf[:], T.ua[:], T.base[:], A.add, ["ua", "base"], ["uf"]),
-            "uoff": lambda: cp(T.uoff[:], T.uf[:], ["uf"], ["uoff"]),
-            "item": lambda: ts(T.item[:], HF, 12582912.0, 12582912.0, A.add, A.subtract, ["pY:h"], ["item"]),
-            "ub": ub, "scat": scat, "fmax": fmax,
-            "phigh": lambda: tt(T.phigh[:], phi, tP, A.subtract, [pk_, "pV:t"], ["phigh"]),
-            "br": lambda: ts(bR, T.q4[:, 0::2], 32768.0, None, A.is_ge, None, ["q4"], ["pV:br"]),
-            "tr": lambda: tt(tR, dr, bR, A.mult, [rk, "pV:br"], ["pV:tr"]),
-            "d1": lambda: tt(T.d1[:], T.phigh[:], PL, A.subtract, ["phigh", "pV:pl"], ["d1"]),
-            "rlow": rlow,
-            "pa": lambda: ts(PA, PL, AP_, None, A.add, None, ["pV:pl", "pS:a"], ["pV:pa"]),
-            "prod": lambda: tt(T.prod[:], T.rlow[:, :, k:k + 8], PL, A.mult, ["rlowa", "rlowb", "pV:pl"], ["prod"]),
+            "s1": lambda: scan(T.s1[:, 1:129], T.low[:], K, -1.0e9, A.max, A.max, ["low", "pK:k"], ["s1"]),
+            "keep": lambda: tt(T.keep[:], K, T.s1[:, 0:128], A.is_lt, ["pK:k", "s1"], ["keep"]),
+            "sy": lambda: scan(T.sy[:], T.keep[:], DL, 0.0, A.mult, A.add, ["keep", "pS:dl"], ["sy"]),
+            "yoff": lambda: ts(T.yoff[:], T.sy[:, 15::16], 2048.0, None, A.add, None, ["sy"], ["yoff"]),
+            "y": lambda: act(T.y[:], win.indirect(T.yoff[:, 0:8]), ACT.Copy, ["tab", "yoff"], ["y"]),
+            "zd": zd, "hf": hf, "zsend": zsend, "u": u,
+            "zabs": lambda: act(zo, Dp, ACT.Abs, ["pS:d"], ["zo%d" % s]),
+            "wp": lambda: tt(T.wp[:], T.s1[:, :].indirect(T.bc64[:, 0:4]), blk(T.jin, s, 64), A.add, ["s1", "bc64", jk], ["wp"]),
+            "bb": lambda: ts(T.bb[:], T.wp[:], 3, 1, A.arith_shift_right, A.bitwise_and, ["wp"], ["bb"]),
+            "t": lambda: tt(tP, T.bb[:], DP, A.mult, ["bb", "pX:dp"], ["pV:t"]),
+            "pl": lambda: tt(T.pl_[:], pv(T.pin, s, 0, 0), tP, A.add, [pk_, "pV:t"], ["pl"]),
+            "ph": lambda: tt(T.ph[:], pv(T.pin, s, 1, 0), tP, A.subtract, [pk_, "pV:t"], ["ph"]),
+            "poff": lambda: ts(T.poff[:], T.pl_[:], 2048.0, None, A.add, None, ["pl"], ["poff"]),
+            "t8": lambda: act(T.t8[:], SZ, ACT.Identity, ["pK:k", "thr"], ["t8"], -1.0, T.thr[:, 0:1]),
+            "wr": lambda: tt(T.wr[:], T.s1[:, :].indirect(T.bc128[:, 0:8]), blk(T.lin, s, 128), A.add, ["s1", "bc128", lk], ["wr"]),
+            "q4": lambda: ts(T.q4[:], T.wr[:], 15, None, A.bitwise_and, None, ["wr"], ["q4"]),
+            "jn": lambda: ts(blk(T.jout, s, 64), T.wr[:, 0::2], 7, None, A.bitwise_and, None, ["wr"], ["jn%d" % s]),
+            "h": lambda: ts(HH, T.q4[:], 7.0, BIGH, A.is_ge, A.mult, ["q4"], ["pV:h"]),
+            "n16": lambda: ts(T.n16[:], T.q4[:], 15.0, -16.0, A.is_equal, A.mult, ["q4"], ["n16"]),
+            "thrb": lambda: act(T.thrb[:], T.t8[:, :].indirect(T.bc8[:, 0:8]), ACT.Copy, ["t8", "bc8"], ["thrb"]),
+            "far": lambda: tt(T.far[:], K, T.thrb[:], A.is_le, ["pK:k", "thrb"], ["far"]),
+            "flag": lambda: tt(T.flag[:], T.far[:], HH, A.is_gt, ["far", "pV:h"], ["flag"]),
+            "r8": r8, "lsend": lsend,
+            "lo": lambda: tt(blk(T.lout, s, 128), T.q4[:], R8, A.add, ["q4", "pX:r8"], ["lo%d" % s]),
+            "qi": lambda: tt(T.qi[:], U, T.negi[:], A.add, ["pX:u", "negi"], ["qi"]),
+            "fr": lambda: tt(T.fr[:], U, T.qi[:], A.subtract, ["pX:u", "qi"], ["fr"]),
+            "uoff": lambda: ts(T.uoff[:], T.fr[:], 32.0, 15.5, A.mult, A.add, ["fr"], ["uoff"]),
+            "item": lambda: ts(T.item[:], HF, 12582912.0, 12582912.0, A.add, A.subtract, ["pS:h"], ["item"]),
+            "scat": scat, "fsa": lambda: fs(0), "fsb": lambda: fs(1),
+            "plu": lambda: act(T.plu[:], T.pl_[:], ACT.Identity, ["pl"], ["plu"], bias=2048.0),
+            "phu": lambda: act(T.phu[:], T.ph[:], ACT.Identity, ["ph"], ["phu"], bias=2048.0),
+            "pa": lambda: act(T.pa[:], T.pl_[:], ACT.Identity, ["pl", "af"], ["pa"], bias=T.af[:, 0:1]),
+            "tr": lambda: tt(tR, T.pV[:, 384:512:2], dr, A.mult, [rk, "pV:h"], ["pV:tr"]),
+            "rlow": lambda: tt(tR, rlo, tR, A.add, [rk, "pV:tr"], ["pV:tr"]),
+            "d1": lambda: tt(D1, T.ph[:], T.pl_[:], A.subtract, ["ph", "pl"], ["pV:d1"]),
+            "prod": lambda: tt(T.prod[:], T.plu[:], tR, A.mult, ["plu", "pV:tr"], ["prod"]),
             "sh": lambda: ts(T.sh[:], T.prod[:], 5, None, A.arith_shift_right, None, ["prod"], ["sh"]),
-            "sm": lambda: tt(T.sm[:], T.sh[:], PA if s else PL, A.add, ["sh", "pV:pa", "pV:pl"], ["sm"]),
+            "sm": lambda: tt(T.sm[:], T.sh[:], T.pa[:], A.add, ["sh", "pa"], ["sm"]),
             "nw": lambda: ts(T.nw[:], T.sm[:], 4095, None, A.bitwise_and, None, ["sm"], ["nw"]),
-            "d2": lambda: tt(T.d2[:], T.nw[:], T.phigh[:], A.subtract, ["nw", "phigh"], ["d2"]),
-            "lf": lambda: ts(LF, Fp, T.thr[:, 0:1], None, A.is_le, None, ["pF:f", "thr"], ["pV:lf"]),
-            "m1": lambda: tt(T.m1[:], T.d1[:], LF, A.mult, ["d1", "pV:lf"], ["m1"]),
-            "t2": lambda: tt(tR, T.d2[:], LF, A.mult, ["d2", "pV:lf"], ["pV:tr"]),
+            "d2": lambda: tt(D2, T.nw[:], T.phu[:], A.subtract, ["nw", "phu"], ["pV:d2"]),
+            "lf": lambda: ts(T.lf[:], Fp, T.thr[:, 0:1], None, A.is_le, None, ["pS:f", "thr"], ["lf"]),
+            "m1": lambda: tt(M1, T.lf[:], D1, A.mult, ["pV:d1", "lf"], ["pV:m1"]),
+            "m2": lambda: tt(M2, T.lf[:], D2, A.mult, ["pV:d2", "lf"], ["pV:m2"]),
             "po": po, "cnt": cnt,
+            "rsend": lambda: s + 2 < ST and send_r(s + 2),
         }
-        skip = (("loa", "lm", "lo", "cnt") if last else ()) + (("pa",) if s == 0 else ())
-        for n in ORDER:
-            if n not in skip:
+        for hh in range(2):
+            call["v%d" % hh] = lambda hh=hh: act(T.v[:, 512 * hh:512 * hh + 512], win.indirect(T.poff[:, 32 * hh:32 * hh + 32]), ACT.Copy,
+                                                 ["tab", "poff"], ["v%d" % hh])
+            call["fd%d" % hh] = lambda hh=hh: fd(hh)
+        for k in range(4):
+            call["fa%d" % k] = lambda k=k: fa(k)
+        for n in (("lsend", "cnt", "jn") if last else ()):
+            call[n] = lambda: None
+        return call
+
+    def run(order, call):
+        for n in order:
+            if n in call:
+                name[0] = n
                 call[n]()
 
     send_r(1)
-    gather_r(0)
-    ztiles(0)
+    run(FIRST, near_calls(0))
     for s in range(ST):
-        nearest(s)
-        step(s)
+        call = step_calls(s)
+        if s + 1 < ST:
+            call.update(near_calls(s + 1))
+        run(ORDER, call)
 
+    name[0] = "tail"
     s = ST - 1
     rlo, dr = blk(T.rf, s, 128, 0, 64), blk(T.rf, s, 128, 64, 128)
-    ts(T.bb[:], T.ls[:, 0::2], 15, 1, A.arith_shift_right, A.bitwise_and, ["ls"], ["bb"])
-    tt(T.sx[:], T.mm8[:], T.ee[:], A.subtract, ["mm8", "ee"], ["sx"])
-    ts(T.pk[:], blk(T.pout, s, 128), 4096.0, None, A.mult, None, ["poa7", "po7"], ["pk"])
-    tt(tP, T.bb[:], dr, A.mult, ["bb"], ["pV:t"])
-    tt(T.d1[:], rlo, dr, A.add, [], ["d1"])
+    C7 = T.pV[:, 128:256]
+    ts(T.h[:, 0:64], T.lout[:, 128 * s:128 * s + 128:2], 6.0, BIGH, A.is_ge, A.mult, ["lo%d" % s], ["h"])
+    tt(T.sx[:], T.mm8[:], T.q4[:, 0::2], A.subtract, ["mm8", "q4"], ["sx"])
+    ts(T.pk[:], T.pout[:, 16 * s:16 * s + 16, 1:9], 2048.0, 4096.0, A.add, A.mult, ["po0%d" % s, "po1%d" % s], ["pk"])
+    tt(tP, T.h[:, 0:64], dr, A.mult, ["h"], ["pV:t"])
+    ts(T.d2[:], dr, BIGH, None, A.mult, None, [], ["d2"])
     for b in range(3):
-        ts(T.bits[:, 64 * b:64 * b + 64], T.sx[:], 12 + b, 1, A.arith_shift_right, A.bitwise_and, ["sx"], ["bits%d" % b])
-    tt(T.pV[:, 128:192], rlo, tP, A.add, ["pV:t"], ["pV:c7"])
-    tt(T.pV[:, 192:256], T.d1[:], tP, A.subtract, ["d1", "pV:t"], ["pV:c7b"])
+        ts(T.bits[:, 64 * b:64 * b + 64], T.sx[:], b, 1, A.arith_shift_right, A.bitwise_and, ["sx"], ["bits%d" % b])
+    tt(T.d1[:], rlo, T.d2[:], A.add, ["d2"], ["d1"])
+    tt(T.pV[:, 128:192], rlo, tP, A.add, ["pV:t"], ["pV:d1"])
+    tt(T.pV[:, 192:256], T.d1[:], tP, A.subtract, ["d1", "pV:t"], ["pV:d2"])
     cur, ck, oth, ok = T.xa, "xa", T.xb, "xb"
     for e in range(2):
-        tt(cur[:, :, 8 * e:8 * e + 8], T.pk[:], C7, A.add, ["pk", "pV:c7", "pV:c7b"], [ck + str(e)])
+        tt(cur[:, :, 8 * e:8 * e + 8], T.pk[:], C7, A.add, ["pk", "pV:d1", "pV:d2"], [ck + str(e)])
     for b in range(3):
         k = 1 << b
-        tt(T.pV[:, 0:128], cur[:, :, k:k + 8], cur[:, :, 0:8], A.subtract, [ck + "0", ck + "1"], ["pV:t", "pV:pl"])
+        tt(T.pV[:, 0:128], cur[:, :, k:k + 8], cur[:, :, 0:8], A.subtract, [ck + "0", ck + "1"], ["pV:t", "pV:tr"])
         for h in range(2):
             tt(T.pV[:, 256 + 64 * h:320 + 64 * h], T.pV[:, 64 * h:64 * h + 64], T.bits[:, 64 * b:64 * b + 64], A.mult,
-               ["pV:t", "bits%d" % b], ["pV:tr" if h else "pV:br"])
+               ["pV:t", "bits%d" % b], ["pV:m2" if h else "pV:m1"])
         if b < 2:
             for e in range(2):
-                tt(oth[:, :, 8 * e:8 * e + 8], cur[:, :, 0:8], T.pV[:, 256:384], A.add, [ck + "0", "pV:br", "pV:tr"], [ok + str(e)])
+                tt(oth[:, :, 8 * e:8 * e + 8], cur[:, :, 0:8], T.pV[:, 256:384], A.add, [ck + "0", "pV:m1", "pV:m2"], [ok + str(e)])
             cur, ck, oth, ok = oth, ok, cur, ck
         else:
             for e in range(2):
                 for h in range(2):
                     tt(T.dup[:, e::2, 8 * h:8 * h + 8], cur[:, 8 * h:8 * h + 8, 0:8], T.pV[:, 256 + 64 * h:320 + 64 * h], A.add,
-                       [ck + "0", "pV:br", "pV:tr"], ["fin%d%d" % (e, h)])
+                       [ck + "0", "pV:m1", "pV:m2"], ["fin%d%d" % (e, h)])
     op("V", lambda: g.vector.transpose(T.tr[:], T.dup[:]), ["fin00", "fin01", "fin10", "fin11"], ["tr"])
     cp(T.wi[:], T.tr[:, :].indirect(T.tl[:, 0:8]), ["tr"], ["wi"])
     ts(T.hi3[:], T.wi[:], 12, None, A.arith_shift_right, None, ["wi"], ["hi3"])

@@ -3,13 +3,17 @@ from concourse.bass import DstId, RemoteDMATransfer
 
 ST, HOP, NR = 8, 3, 8
 F32, BF, F16, I32, U16 = "float32", "bfloat16", "float16", "int32", "uint16"
-AW = 136
-CH = (("S", 0, 32), ("V", 32, 48), ("V", 48, 64), ("S", 64, 96), ("S", 96, 112), ("S", 112, 128))
-MX = ((0, 32, 0, 1), (32, 64, 0, 1), (64, 96, 0, 2), (96, 128, 0, 2), (64, 96, 1, 2), (96, 128, 1, 2))
-ORDER = ("s1 wp keep bb sy t8 t thrb yoff y zd pl wr u plu poff q4 h far n16 tr v0 fd0 jn zabs zsend v1 hf pa qi rlow ph phu fr prod flag fa2 sh "
-         "fa0 fd1 uoff fa1 item d1 r8 scat init fa3 sm lo nw lsend fsa g2 d2 fsb zt1 lf g1 m1 m2 zt0 g3 x2 po rsend g5 g4 sa1 x3 sm1 g0 sa0 sg x1 "
-         "cnt xx qb x0 x5 lab x4 sm0 sm2 sl thr af dp dl").split()
-FIRST = "g0 g1 g2 init zt0 zt1 lab sg sl dl dp g3 g4 x0 x1 sa0 sm0 g5 sa1 x2 x3 sm1 x4 x5 sm2".split()
+CH = (("S", 0, 8), ("V", 8, 13), ("S", 13, 16), ("S", 16, 24), ("S", 24, 29), ("S", 29, 32))
+CH0 = (2,)
+CV = (("S", 0, 16), ("S", 16, 32), ("S", 32, 48), ("V", 48, 64))
+ORDER = ("s1 sl af wp qb xx thr zn keep bb dl sy dp t t8 thrb yoff y hf pl pa wr plu poff v0 zd u v1 zr zsend v3 q4 ph fd0 v2 item phu h fd1 far "
+         "fa0 qi fa2 tr n16 init fr rlow flag uoff r8 fa1 jn prod sh scat fa3 sm d1 lo lsend fsa fsb nw g1 g2 d2 sa2 zt1 lf zt0 m1 m2 g0 sz sa1 cnt "
+         "x2 sa0 g3 sm2 sa3 po x0 sm0 x1 x3 sm1 g4 g5 x4 sa4 rsend lab x5 sm3 sa5 sm4 sm5 sg").split()
+FIRST = "zz init lab sg zt0 zt1 sz g0 g1 g2 sa1 x1 sm1 g3 sa0 sa2 x0 sm0 x2 sm2 g4 sa3 x3 sm3 g5 sa4 x4 sm4 sa5 x5 sm5 th".split()
+LAST = ("s1 xx zn ra qb thr sl dl keep t8 wp wr bb sy dp t q4 yoff thrb y af pl plu ph h poff u v0 n16 hf tr zd far v1 v2 fd0 v3 fd1 pa phu rd "
+        "qi rlow flag fr zr fa2 prod zsend r8 fa0 item uoff scat d1 lo sh sx wb sm sx7 fa1 fsa fa3 fsb rt nw rb lf mk0 m1 d2 ro m2 mk1 po "
+        "sf10 sf00 sf01 sf11 back0 back1 out0 out1").split()
+LATE = "xx qb af thr sl dp dl zn".split()
 
 
 def _sb(shape, d):
@@ -17,9 +21,10 @@ def _sb(shape, d):
 
 
 SCRATCH = {
-    "tab": _sb([4096], BF), "a": _sb([AW * 8 * 16], BF), "mx": _sb([128, 16], BF), "v": _sb([1024], BF), "mf": _sb([64, 16], BF),
+    "tab": _sb([4096], BF), "a": _sb([2048], BF), "mx": _sb([2048], BF), "zin": _sb([256 * 8], BF), "zp": _sb([8], U16), "zq": _sb([8], U16),
+    "prh": _sb([128], F16), "e0": _sb([144], F16), "e1": _sb([144], F16), "v": _sb([1024], BF), "mf": _sb([64, 16], BF),
     "pli": _sb([128], I32), "pri": _sb([128], I32), "thi": _sb([4], I32),
-    "zout": _sb([128 * 8], BF), "lin": _sb([128 * 8], BF), "lout": _sb([128 * 8], BF), "jin": _sb([64 * 8], I32), "jout": _sb([64 * 8], I32),
+    "zout": _sb([128 * 8], BF), "dd": _sb([128], BF), "lin": _sb([128 * 8], BF), "lout": _sb([128 * 8], BF), "jin": _sb([64 * 8], I32), "jout": _sb([64 * 8], I32),
     "pin": _sb([16 * 8, 10], F16), "pout": _sb([16 * 8, 10], F16), "sl": _sb([16, 10], F16), "roff": _sb([128 * 8], U16), "rf": _sb([128 * 8], F32),
     "ai": _sb([144], I32), "ip": _sb([4], I32), "pm": _sb([8], I32), "col": _sb([8], F32), "ti": _sb([144], I32), "lab0": _sb([128], BF),
     "za": _sb([144], BF), "zm": _sb([144], BF), "zu": _sb([144], BF), "idb": _sb([128], BF), "idn": _sb([128], BF), "idh": _sb([128], BF),
@@ -27,7 +32,7 @@ SCRATCH = {
     "f1": _sb([128], F16), "f1n": _sb([128], F16), "fh": _sb([128], F16), "fhn": _sb([128], F16), "bones": _sb([128], F32),
     "off": _sb([144], BF), "c2": _sb([128], BF), "cq": _sb([128], BF), "cu": _sb([8], BF), "c1": _sb([128], BF), "low": _sb([128], F32),
     "bc128": _sb([8], U16), "bc64": _sb([8], U16), "bc8": _sb([8], U16), "tl": _sb([8], U16), "negi": _sb([8], F32), "mm8": _sb([64], F32),
-    "pk": _sb([128], F32), "dup": _sb([16, 16], F32), "tr": _sb([256], F32), "wi": _sb([128], I32), "hi3": _sb([16, 8], I32), "lo3": _sb([16, 8], I32),
+    "pk": _sb([128], F32), "dup": _sb([16, 16], F32), "tr": _sb([512], F32), "wi": _sb([128], I32), "hi3": _sb([16, 8], I32), "lo3": _sb([16, 8], I32),
     "s1": _sb([136], F32), "keep": _sb([128], BF), "wp": _sb([64], I32), "bb": _sb([64], I32), "t8": _sb([8], F32), "h": _sb([128], BF),
     "thrb": _sb([128], F32), "poff": _sb([64], U16), "sy": _sb([128], F32), "yoff": _sb([8], U16), "y": _sb([128], BF),
     "wr": _sb([128], I32), "q4": _sb([128], I32), "flag": _sb([128], BF), "far": _sb([128], BF), "n16": _sb([128], BF),
@@ -36,7 +41,7 @@ SCRATCH = {
     "pl_": _sb([64], F32), "ph": _sb([64], F32), "plu": _sb([64], F32), "phu": _sb([64], F32), "pa": _sb([64], F32),
     "d1": _sb([64], F32), "d2": _sb([64], F32), "lf": _sb([64], F32), "junk": _sb([64], F32),
     "cnt": _sb([4], F32), "af": _sb([4], F32), "qb": _sb([8], BF), "xx": _sb([4], F32), "thr": _sb([4], F32), "th2": _sb([4], F32),
-    "sx": _sb([64], I32), "bits": _sb([192], I32), "xa": _sb([16, 16], F32), "xb": _sb([16, 16], F32),
+    "sx": _sb([64], I32), "mk": _sb([512], BF), "part": _sb([2048], F16),
     "op": _sb([128], F32), "orr": _sb([128], F32),
     "pK": ("psum", [128, 512], F32), "pA": ("psum", [128, 32, 16], F32), "pB": ("psum", [128, 32, 16], F32), "pS": ("psum", [128, 512], F32),
     "pC": ("psum", [128, 32, 16], F32), "pD": ("psum", [128, 32, 16], F32), "pX": ("psum", [128, 512], F32), "pV": ("psum", [128, 512], F32),
@@ -162,8 +167,8 @@ def rank_program(g, core, T, topo):
     def blk(t, s, n, a=0, b=None):
         return t[:, n * s + a:n * s + (n if b is None else b)]
 
-    def zin(s, a=0, b=8):
-        return T.a[:, 16 * (AW * s + 128 + a):16 * (AW * s + 128 + b)]
+    def zin(s, a=0, b=128):
+        return blk(T.zin, s, 256, a, b)
 
     def pv(t, s, h, k):
         return t[:, 16 * s + 8 * h:16 * s + 8 * h + 8, k:k + 8]
@@ -177,75 +182,86 @@ def rank_program(g, core, T, topo):
 
     dma("Y", T.pri[:], T.pr[:], (), ["pri"])
     dma("S", T.pli[:], T.pl[:], (), ["pli"])
+    dma("Y", zin(0), T.z0[:], (), ["zn0"])
     dma("Y", T.tab[:], T.xt[:], (), ["tab"])
     dma("S", T.thi[:, 0:1], T.th[:], (), ["thi"])
-    dma("S", zin(0), T.z0[:], (), ["z0"])
 
     op("G", lambda: g.iota(T.ip[:, 0:1], [[0, 1]], 0, 1), (), ["ip"])
     op("G", lambda: g.iota(T.ai[:], [[1, 144]], 0, 0), (), ["ai"])
     op("G", lambda: g.iota(T.lab0[:], [[0, 8], [1, 8], [8, 2]], -2, 0, allow_small_or_imprecise_dtypes=True), (), ["lab0"])
     op("G", lambda: g.iota(T.sx[:], [[0, 8], [1, 8]], 7, 0), (), ["sx"])
-    op("G", lambda: g.iota(T.ti[:, 128:144], [[-1, 8], [0, 2]], 0, 0), (), ["tib"])
-    for t, c in (("c2", -2.0), ("cq", -0.25), ("cu", -15.5 / 32), ("c1", -1.0), ("low", -1.0e9), ("junk", 0.0), ("pk", 0.0)):
+    op("G", lambda: g.iota(T.ti[:, 128:144], [[0, 2], [-1, 8]], 0, 0), (), ["tib"])
+    for t, c in (("c2", -2.0), ("cq", -0.25), ("cu", -15.5 / 32), ("c1", -1.0), ("low", 0.0), ("junk", 0.0)):
         ms(T[t][:], c, [t])
     ms(T.s1[:, 0:8], -1.0e9, ["s1"])
     ms(T.af[:, 0:1], 2048.0, ["af"])
-    for k, m in enumerate((31, 112, 8, 15)):
+    for k, m in enumerate((31, 112, 8, 15, 7)):
         ts(T.pm[:, k:k + 1], T.ip[:, 0:1], m, None, A.bitwise_and, None, ["ip"], ["pm%d" % k])
+    cp(T.col[:, 5:6], T.ip[:, 0:1], ["ip"], ["col5"])
     cp(T.col[:, 0:1], T.pm[:, 0:1], ["pm0"], ["col0"])
     cp(T.col[:, 1:2], T.pm[:, 1:2], ["pm1"], ["col1"])
     ts(T.col[:, 2:3], T.pm[:, 1:2], 15.0, None, A.add, None, ["pm1"], ["col2"])
     ts(T.col[:, 3:4], T.pm[:, 2:3], 2.0, 16.0, A.mult, A.add, ["pm2"], ["col3"])
     cp(T.col[:, 4:5], T.pm[:, 3:4], ["pm3"], ["col4"])
-    cp(T.col[:, 5:6], T.ip[:, 0:1], ["ip"], ["col5"])
-    ts(T.tl[:], T.ai[:, 0:8], 32.0, T.col[:, 0:1], A.mult, A.add, ["ai", "col0"], ["tl"])
+    ts(T.col[:, 6:7], T.pm[:, 2:3], -32.0, T.col[:, 5:6], A.mult, A.add, ["pm2", "col5"], ["col6"])
+    ts(T.col[:, 7:8], T.pm[:, 2:3], 32.0, T.col[:, 5:6], A.mult, A.add, ["pm2", "col5"], ["col7"])
+    ts(T.xx[:, 1:2], T.pm[:, 2:3], 0.125, None, A.mult, None, ["pm2"], ["xx1"])
+    ts(T.xx[:, 3:4], T.pm[:, 3:4], 8.0, None, A.mult, None, ["pm3"], ["xx3"])
     ts(T.idb[:], T.ai[:, 0:128], T.col[:, 5:6], None, A.is_equal, None, ["ai", "col5"], ["idb"])
-    for t, wgt in (("za", 16.0), ("zm", -32.0), ("zu", 1.0 / 32)):
-        ts(T[t][:], T.ai[:], T.col[:, 2:3], wgt, A.is_equal, A.mult, ["ai", "col2"], [t])
-    ts(T.ti[:, 0:128], T.ai[:, 0:128], 4, None, A.arith_shift_right, None, ["ai"], ["ti"])
-    cp(T.pout[:, :, 9], T.pk[:], ["pk"], ["pz"])
-    cp(T.pin[:, 0:16, 9], T.junk[:, 0:16], ["junk"], ["p0z"])
-    cp(T.sl[:, :, 8], T.junk[:, 0:16], ["junk"], ["slz"])
-    ts(T.off[:], T.ti[:], 2.0 ** 18, None, A.mult, None, ["ti", "tib"], ["off"])
+    ts(T.e0[:], T.ai[:], -8.0, T.col[:, 6:7], A.add, A.is_equal, ["ai", "col6"], ["e0"])
+    ts(T.e1[:], T.ai[:], 248.0, T.col[:, 7:8], A.add, A.is_equal, ["ai", "col7"], ["e1"])
+    ts(T.za[:], T.ai[:], T.col[:, 2:3], 16.0, A.is_equal, A.mult, ["ai", "col2"], ["za"])
+    ts(T.xx[:, 2:3], T.pm[:, 4:5], 16.0, T.xx[:, 1:2], A.mult, A.add, ["pm4", "xx1"], ["xx2"])
+    ts(T.tl[:], T.ai[:, 0:8], 32.0, T.col[:, 0:1], A.mult, A.add, ["ai", "col0"], ["tl"])
+    cp(T.pout[:, :, 9], T.low[:], ["low"], ["pz"])
+    for t, src, wgt in (("zm", "za", -2.0), ("zu", "za", 1.0 / 512), ("idn", "idb", -1.0), ("idh", "idb", 0.5), ("id8", "idb", 8.0),
+                        ("id8n", "idb", -8.0), ("idq", "idb", 0.125), ("idqn", "idb", -0.125)):
+        act(T[t][:], T[src][:], ACT.Copy, [src], [t], wgt)
 
+    ts(T.prh[:], T.pri[:], -2048.0, None, A.add, None, ["pri"], ["prh"])
+    for h in range(2):
+        for b in range(2):
+            for c in range(4):
+                mm(T.pX[:, 64 * h + c:64 * h + 64:4], T["e%d" % h][:, 8 - 8 * (b - h):136 - 8 * (b - h)], T.prh[:, 32 * c + 16 * b:32 * c + 16 * b + 16],
+                   h + b + c == 0, h + b + c == 5, ["e%d" % h, "prh"], ["pX:ro"])
     ts(T.pk[:], T.pli[:], 4096.0, None, A.mult, None, ["pli"], ["pk"])
+    ts(T.ti[:, 0:128], T.ai[:, 0:128], 4, None, A.arith_shift_right, None, ["ai"], ["ti"])
+    ts(T.q4[:], T.ai[:, 0:128], 112, None, A.bitwise_and, None, ["ai"], ["q4"])
     for e in range(2):
         tt(T.dup[:, e::2, :], T.pk[:], T.pri[:], A.add, ["pk", "pri"], ["dup%d" % e])
-    op("V", lambda: g.vector.transpose(T.tr[:], T.dup[:]), ["dup0", "dup1"], ["tr"])
-    cp(T.wi[:], T.tr[:, :].indirect(T.tl[:, 0:8]), ["tr", "tl"], ["wi"])
+    ts(T.roff[:, 0:128], T.pX[:, 0:128], 2048.0, None, A.add, None, ["pX:ro"], ["ro0"])
+    ts(T.off[:], T.ti[:], 2.0 ** 18, None, A.mult, None, ["ti", "tib"], ["off"])
+    op("V", lambda: g.vector.transpose(T.tr[:, 0:256], T.dup[:]), ["dup0", "dup1"], ["tr0"])
+    ts(T.bones[:], T.q4[:], T.col[:, 1:2], None, A.is_equal, None, ["q4", "col1"], ["bones"])
+    ts(T.zp[:], T.ai[:, 0:8], 2.0, T.xx[:, 2:3], A.mult, A.add, ["ai", "xx2"], ["zp"])
+    ts(T.zq[:], T.ai[:, 0:8], T.xx[:, 3:4], None, A.add, None, ["ai", "xx3"], ["zq"])
+    cp(T.wi[:], T.tr[:, 0:256].indirect(T.tl[:, 0:8]), ["tr0", "tl"], ["wi"])
+    for t, wgt in (("f1", 1.0), ("f1n", -1.0), ("fh", 0.5), ("fhn", -0.5)):
+        ts(T[t][:], T.idb[:], wgt, None, A.mult, None, ["idb"], [t])
     ts(T.lo3[:], T.wi[:], 4095, None, A.bitwise_and, None, ["wi"], ["lo3"])
     ts(T.hi3[:], T.wi[:], 12, None, A.arith_shift_right, None, ["wi"], ["hi3"])
-    for h in range(2):
-        cp(T.roff[:, 64 * h:64 * h + 64], T.lo3[:, h::2, :], ["lo3"], ["ro0h%d" % h])
-    cp(T.rf[:, 0:64], T.lo3[:, 0::2, :], ["lo3"], ["rf0a"])
+    cp(T.pin[:, 0:16, 9], T.junk[:, 0:16], ["junk"], ["p0z"])
+    cp(T.sl[:, :, 8], T.junk[:, 0:16], ["junk"], ["slz"])
     tt(T.d1[:], T.lo3[:, 1::2, :], T.lo3[:, 0::2, :], A.subtract, ["lo3"], ["d1"])
+    cp(T.rf[:, 0:64], T.lo3[:, 0::2, :], ["lo3"], ["rf0a"])
     for h in range(2):
         ts(pv(T.pin, 0, h, 1), T.hi3[:, h::2, :], -2048.0, None, A.add, None, ["hi3"], ["p0a%d" % h])
         ts(T.pin[:, 8 * h:8 * h + 8, 0], T.hi3[:, h::2, 7], -2048.0, None, A.add, None, ["hi3", "p0z"], ["p0b%d" % h])
     ts(T.rf[:, 64:128], T.d1[:], 1.0 / BIGH, None, A.mult, None, ["d1"], ["rf0"])
-    writer["ro0"] = writer["ro0h1"]
     writer["p0"] = writer["p0b1"]
-
-    for t, wgt in (("idn", -1.0), ("idh", 0.5), ("id8", 8.0), ("id8n", -8.0), ("idq", 0.125), ("idqn", -0.125),
-                   ("f1", 1.0), ("f1n", -1.0), ("fh", 0.5), ("fhn", -0.5)):
-        ts(T[t][:], T.ai[:, 0:128], T.col[:, 5:6], wgt, A.is_equal, A.mult, ["ai", "col5"], [t])
     ts(T.bc128[:], T.ai[:, 0:8], 16.0, 16.0, A.mult, A.add, ["ai"], ["bc128"])
     ts(T.bc64[:], T.ai[:, 0:8], 32.0, T.col[:, 3:4], A.mult, A.add, ["ai", "col3"], ["bc64"])
     cp(T.bc8[:], T.ai[:, 0:8], ["ai"], ["bc8"])
     ts(T.negi[:], T.ai[:, 0:8], -16.0, T.col[:, 4:5], A.mult, A.subtract, ["ai", "col4"], ["negi"])
-    ts(T.wi[:], T.ai[:, 0:128], 112, None, A.bitwise_and, None, ["ai"], ["wi"])
     ts(T.jin[:, 0:64], T.sx[:], 7, None, A.bitwise_and, None, ["sx"], ["j0"])
     cp(T.lin[:, 0:128], T.lab0[:], ["lab0"], ["l0"])
-    ts(T.thr[:, 0:1], T.thi[:, 0:1], 1.0, -16.0, A.add, A.mult, ["thi"], ["thr"])
-    ts(T.th2[:, 0:1], T.thi[:, 0:1], 1.0 + 32 * 192, -16.0, A.add, A.mult, ["thi"], ["th2"])
-    ts(T.bones[:], T.wi[:], T.col[:, 1:2], None, A.is_equal, None, ["wi", "col1"], ["bones"])
     ts(T.mm8[:], T.sx[:], 16.0, None, A.add, None, ["sx"], ["mm8"])
 
     def sel(t, r):
         return t[:, 15 - r:143 - r]
 
-    K, SZ = T.pK[:, 0:128], T.pK[:, 129:144:2]
-    Dp, HF, Fp, AP_, DL = T.pS[:, 0:128], T.pS[:, 128:256], T.pS[:, 256:320], T.pS[:, 320:321], T.pS[:, 384:512]
+    K, SZ = T.pK[:, 0:128], T.pK[:, 128:136]
+    HF, Fp, AP_, DL = T.pS[:, 128:256], T.pS[:, 256:320], T.pS[:, 320:321], T.pS[:, 384:512]
     U, R8, DP, SG = T.pX[:, 0:8], T.pX[:, 128:256], T.pX[:, 256:320], T.pX[:, 320:384]
     tP, tR, D1, D2, M1, M2 = (T.pV[:, 64 * k:64 * k + 64] for k in range(6))
     HH = T.pV[:, 384:512]
@@ -254,24 +270,23 @@ def rank_program(g, core, T, topo):
     win = T.tab[:, :]
     outs = []
 
+    def gather(q, out, off, r, w):
+        if q == "V":
+            cp(out, win.indirect(off), ["tab", r], [w])
+        else:
+            act(out, win.indirect(off), ACT.Copy, ["tab", r], [w])
+
     def send_r(s):
         d = (rank + HOP * s) % NR
-        send(d, [(blk(T.roff, s, 128), blk(T.roff, 0, 128))], "ar%d" % s, ["ro0h0", "ro0h1"])
+        send(d, [(blk(T.roff, s, 128), blk(T.roff, 0, 128))], "ar%d" % s, ["ro0"])
         send(d, [(blk(T.rf, s, 128), blk(T.rf, 0, 128))], "ar%d" % s, ["rf0a", "rf0"])
 
     def near_calls(s):
-        zk, lk, pk_, c0 = "z%d" % s, "l%d" % s, "p%d" % s, AW * s
+        zk, lk, pk_ = "z%d" % s, "l%d" % s, "p%d" % s
 
-        def parts(lo_, hi_):
-            return ["a%d" % k for k, c in enumerate(CH) if c[1] < hi_ and c[2] > lo_]
-
-        def gather(k):
+        def right(k):
             q, lo_, hi_ = CH[k]
-            src = win.indirect(blk(T.roff, s, 128, lo_, hi_))
-            if q == "V" or (s == 0 and k == 4):
-                cp(T.a[:, 16 * (c0 + lo_):16 * (c0 + hi_)], src, ["tab", "ro%d" % s], ["a%d" % k])
-            else:
-                act(T.a[:, 16 * (c0 + lo_):16 * (c0 + hi_)], src, ACT.Copy, ["tab", "ro%d" % s], ["a%d" % k])
+            gather("V" if s == 0 and k in CH0 else q, T.a[:, 64 * lo_:64 * hi_], blk(T.roff, s, 128, 4 * lo_, 4 * hi_), "ro%d" % s, "a%d" % k)
 
         def init():
             mm(T.pK[:, 0:144], T.idb[:], T.off[:], True, False, ["idb", "off"], ["pK:k"])
@@ -279,23 +294,25 @@ def rank_program(g, core, T, topo):
 
         def ztile(hh):
             for m in range(8):
-                mm(tiles[hh][0][:, m::8, :], T.idb[:], zin(s, 4 * hh, 4 * hh + 4), True, True, ["idb", zk], [tiles[hh][1]])
+                mm(tiles[hh][0][:, :, m::8], T.idb[:], zin(s, 128 + 64 * hh, 192 + 64 * hh), True, True, ["idb", zk], [tiles[hh][1]])
 
         def big(k):
-            lo_, hi_, r0, n = MX[k]
-            t = tiles[lo_ // 32 % 2]
-            tt(T.mx[:, lo_:hi_, r0::n], T.a[:, 16 * (c0 + lo_) + r0:16 * (c0 + hi_):n], t[0][:, lo_ % 32:(hi_ - 1) % 32 + 1, r0::n], A.max,
-               parts(lo_, hi_) + [t[1]], ["mx%d" % k])
+            _, lo_, hi_ = CH[k]
+            t = tiles[lo_ // 8 % 2]
+            tt(T.mx[:, 64 * lo_:64 * hi_], T.a[:, 64 * lo_:64 * hi_], t[0][:, 4 * (lo_ % 8):4 * ((hi_ - 1) % 8 + 1), :], A.max,
+               ["a%d" % k, t[1]], ["mx%d" % k])
 
-        def sum_a(h):
+        def sums(k, t, w_, key, stop):
+            for b in range(CH[k][1], CH[k][2]):
+                mm(T.pK[:, b // 16:128:2], sel(T[w_], b % 16), blk(t, b, 64), False, stop and b == CH[k][2] - 1, [key + str(k), w_], ["pK:k"])
+
+        def sz():
             for r in range(16):
-                mm(T.pK[:, h:128 + 16 * h:2], sel(T.za, r), T.a[:, 16 * (c0 + 64 * h) + r:16 * (c0 + 64 + 72 * h):16], False, False,
-                   parts(64 * h, 64 * h + 64) + [zk if h else "za"], ["pK:k"])
+                mm(SZ, sel(T.za, r), zin(s, 128 + 8 * r, 136 + 8 * r), False, False, ["za", zk], ["pK:k"])
 
-        def sum_m(h, r0, n):
-            r_ = ["mx%d" % k for k, c in enumerate(MX) if c[0] // 64 == h and (c[3] == 1 or n == 1 or c[2] == r0)]
-            for r in range(r0, 16, n):
-                mm(T.pK[:, h:128:2], sel(T.zm, r), T.mx[:, 64 * h:64 * h + 64, r], False, h == 1 and r == 15, r_ + ["zm"], ["pK:k"])
+        def th():
+            ts(T.thr[:, 0:1], T.thi[:, 0:1], 1.0, -16.0, A.add, A.mult, ["thi"], ["thr"])
+            ts(T.th2[:, 0:1], T.thi[:, 0:1], 1.0 + 32 * 192, -16.0, A.add, A.mult, ["thi"], ["th2"])
 
         def dp():
             mm(DP, T.f1[:], pv(T.pin, s, 1, 0), True, False, ["f1", pk_], ["pX:dp"])
@@ -321,24 +338,30 @@ def rank_program(g, core, T, topo):
         call = {
             "init": init, "dp": dp, "sg": sg, "sl": sl, "dl": dl,
             "lab": lambda: mm(K, T.idn[:], blk(T.lin, s, 128), False, False, ["idn", lk], ["pK:k"]),
-            "sm0": lambda: sum_m(0, 0, 1), "sm1": lambda: sum_m(1, 0, 2), "sm2": lambda: sum_m(1, 1, 2),
+            "sz": sz,
+            "zn": lambda: act(zin(s), zin(s, 128, 256).indirect(T.zq[:, 0:8]), ACT.Copy, [zk, "zq"], ["zn%d" % s]),
             "af": lambda: act(T.af[:, 0:1], AP_, ACT.Identity, ["pS:a"], ["af"], bias=2048.0),
             "qb": lambda: act(T.qb[:, 0:1], AP_, ACT.Identity, ["pS:a"], ["qb"], 1.0 / 32, 192 - 15.5 / 32),
             "xx": lambda: act(T.xx[:, 0:1], AP_, ACT.Identity, ["pS:a", "th2"], ["xx"], -16.0, T.th2[:, 0:1]),
             "thr": lambda: act(T.thr[:, 0:1], T.qb[:, 0:1], ACT.Identity, ["qb", "xx"], ["thr"], 512.0, T.xx[:, 0:1]),
         }
         for k in range(len(CH)):
-            call["g%d" % k] = lambda k=k: gather(k)
-        for k in range(len(MX)):
+            call["g%d" % k] = lambda k=k: right(k)
             call["x%d" % k] = lambda k=k: big(k)
+            call["sa%d" % k] = lambda k=k: sums(k, T.a, "za", "a", False)
+            call["sm%d" % k] = lambda k=k: sums(k, T.mx, "zm", "mx", k == len(CH) - 1)
         for h in range(2):
             call["zt%d" % h] = lambda h=h: ztile(h)
-            call["sa%d" % h] = lambda h=h: sum_a(h)
+        if s == 0:
+            for n in ("af", "qb", "xx", "thr", "zn"):
+                del call[n]
+            call["th"] = th
+            call["zz"] = lambda: act(zin(0, 128, 256), zin(0).indirect(T.zp[:, 0:8]), ACT.Copy, ["zn0", "zp"], ["z0"])
         return call
 
     def step_calls(s):
         last = s == ST - 1
-        z, zk, lk, jk, pk_, rk = zin(s), "z%d" % s, "l%d" % s, "j%d" % s, "p%d" % s, "rf%d" % s
+        z, zk, lk, jk, pk_, rk = zin(s), "zn%d" % s, "l%d" % s, "j%d" % s, "p%d" % s, "rf%d" % s
         rlo, dr = blk(T.rf, s, 128, 0, 64), blk(T.rf, s, 128, 64, 128)
         zo = blk(T.zout, s, 128)
 
@@ -354,10 +377,6 @@ def rank_program(g, core, T, topo):
             for r in range(16):
                 mm(U, sel(T.zu, r), T.y[:, r::16], False, r == 15, ["zu", "y"], ["pX:u"])
 
-        def zd():
-            mm(Dp, T.idb[:], T.y[:], True, False, ["y"], ["pS:d"])
-            mm(Dp, T.idn[:], z, False, True, [zk], ["pS:d"])
-
         def hf():
             mm(HF, T.idh[:], T.y[:], True, False, ["idh", "y"], ["pS:h"])
             mm(HF, T.idh[:], z, False, False, [zk], ["pS:h"])
@@ -367,13 +386,14 @@ def rank_program(g, core, T, topo):
             if last:
                 outs.append(dma("Y", T.yz[:], zo, ["zo%d" % s], ()))
             else:
-                send(nxt, [(zin(s + 1), zo)], "az%d" % (s + 1), ["zo%d" % s])
+                send(nxt, [(zin(s + 1, 128, 256), zo)], "az%d" % (s + 1), ["zo%d" % s])
 
         def fd(hh):
             t, key = ftiles[hh]
             for m in range(8):
                 mm(t[:, m::8, :], T.idn[:], T.y[:, 64 * hh:64 * hh + 64], m == 0, False, ["y"], [key])
-            mm(t[:], T.idb[:], T.v[:, 512 * hh:512 * hh + 512], False, True, ["v%d" % hh], [key])
+            mm(t[:], T.idb[:], T.v[:, 512 * hh:512 * hh + 512], False, True,
+               ["v%d" % k for k, c in enumerate(CV) if c[1] < 32 * hh + 32 and c[2] > 32 * hh], [key])
 
         def fa(k):
             hh, r0 = k % 2, 8 * (k // 2)
@@ -390,14 +410,16 @@ def rank_program(g, core, T, topo):
         def scat():
             cp(win.indirect(T.uoff[:, 0:8]), T.item[:], ["uoff", "item"], ["tab"])
             if last:
-                outs.append(dma("S", T.yx[0:64, :], T.tab[0:64, :], ["tab"], ()))
-                outs.append(dma("Y", T.yx[64:128, :], T.tab[64:128, :], ["tab"], ()))
+                outs.append(dma("Y", T.yx[:], T.tab[:], ["tab"], ()))
 
         def po():
             for h, (x, xk, m, mk) in enumerate(((T.pl_, "pl", 4, "pV:m1"), (T.ph, "ph", 5, "pV:m2"))):
+                if last:
+                    for e in range(2):
+                        tt(T.pA[:, 8 * h:8 * h + 8, 8 * e:8 * e + 8], x[:], T.pV[:, 64 * m:64 * m + 64], A.add, [xk, mk], ["pA:0%d%d" % (h, e)])
+                    continue
                 tt(pv(T.pout, s, h, 1), x[:], T.pV[:, 64 * m:64 * m + 64], A.add, [xk, mk, "pz"], ["po%d%d" % (h, s)])
-                if not last:
-                    tt(T.pout[:, 16 * s + 8 * h:16 * s + 8 * h + 8, 0], x[:, 7::8], T.pV[:, 64 * m + 7:64 * m + 64:8], A.add, [xk, mk], ["pw%d%d" % (h, s)])
+                tt(T.pout[:, 16 * s + 8 * h:16 * s + 8 * h + 8, 0], x[:, 7::8], T.pV[:, 64 * m + 7:64 * m + 64:8], A.add, [xk, mk], ["pw%d%d" % (h, s)])
             if not last:
                 send(nxt, [(T.pin[:, 16 * s + 16:16 * s + 32, :], T.pout[:, 16 * s:16 * s + 16, :])], "ap%d" % (s + 1),
                      ["po0%d" % s, "po1%d" % s, "pw0%d" % s, "pw1%d" % s])
@@ -407,13 +429,14 @@ def rank_program(g, core, T, topo):
             mm(AP_, T.bones[:], T.cnt[:, 0:1], True, True, ["bones", "cnt"], ["pS:a"])
 
         call = {
-            "s1": lambda: scan(T.s1[:, 1:129], T.low[:], K, -1.0e9, A.max, A.max, ["low", "pK:k"], ["s1"]),
+            "s1": lambda: scan(T.s1[:, 1:129], T.low[:], K, -1.0e9, A.add, A.max, ["low", "pK:k"], ["s1"]),
             "keep": lambda: tt(T.keep[:], K, T.s1[:, 0:128], A.is_lt, ["pK:k", "s1"], ["keep"]),
             "sy": lambda: scan(T.sy[:], T.keep[:], DL, 0.0, A.mult, A.add, ["keep", "pS:dl"], ["sy"]),
             "yoff": lambda: ts(T.yoff[:], T.sy[:, 15::16], 2048.0, None, A.add, None, ["sy"], ["yoff"]),
             "y": lambda: act(T.y[:], win.indirect(T.yoff[:, 0:8]), ACT.Copy, ["tab", "yoff"], ["y"]),
-            "zd": zd, "hf": hf, "zsend": zsend, "u": u,
-            "zabs": lambda: act(zo, Dp, ACT.Abs, ["pS:d"], ["zo%d" % s]),
+            "hf": hf, "zsend": zsend, "u": u,
+            "zd": lambda: tt(T.dd[:], win.indirect(T.yoff[:, 0:8]), z, A.subtract, ["tab", "yoff", zk], ["dd"]),
+            "zr": lambda: act(zo, T.dd[:] if last else T.dd[:, :].indirect(T.zp[:, 0:8]), ACT.Abs, ["dd", "zp"], ["zo%d" % s]),
             "wp": lambda: tt(T.wp[:], T.s1[:, :].indirect(T.bc64[:, 0:4]), blk(T.jin, s, 64), A.add, ["s1", "bc64", jk], ["wp"]),
             "bb": lambda: ts(T.bb[:], T.wp[:], 3, 1, A.arith_shift_right, A.bitwise_and, ["wp"], ["bb"]),
             "t": lambda: tt(tP, T.bb[:], DP, A.mult, ["bb", "pX:dp"], ["pV:t"]),
@@ -453,14 +476,62 @@ def rank_program(g, core, T, topo):
             "po": po, "cnt": cnt,
             "rsend": lambda: s + 2 < ST and send_r(s + 2),
         }
+        for k in range(len(CV)):
+            call["v%d" % k] = lambda k=k: gather(CV[k][0], T.v[:, 16 * CV[k][1]:16 * CV[k][2]], T.poff[:, CV[k][1]:CV[k][2]], "poff", "v%d" % k)
         for hh in range(2):
-            call["v%d" % hh] = lambda hh=hh: act(T.v[:, 512 * hh:512 * hh + 512], win.indirect(T.poff[:, 32 * hh:32 * hh + 32]), ACT.Copy,
-                                                 ["tab", "poff"], ["v%d" % hh])
             call["fd%d" % hh] = lambda hh=hh: fd(hh)
         for k in range(4):
             call["fa%d" % k] = lambda k=k: fa(k)
-        for n in (("lsend", "cnt", "jn") if last else ()):
-            call[n] = lambda: None
+        return call
+
+    def turn_calls(s):
+        rlo, dr = blk(T.rf, s, 128, 0, 64), blk(T.rf, s, 128, 64, 128)
+        rk = "rf%d" % s
+
+        def masks(t0):
+            for t in range(t0, t0 + 4):
+                ts(blk(T.mk, t, 64), T.wp[:], float(t), None, A.is_equal, None, ["sx7"], ["mk%d" % t])
+
+        def ro():
+            for h, (x, xk, o) in enumerate(((T.d1, "ra", A.add), (T.d2, "rb", A.subtract))):
+                for e in range(2):
+                    tt(T.pA[:, 16 + 8 * h:24 + 8 * h, 8 * e:8 * e + 8], x[:], tP, o, [xk, "pV:t"], ["pA:1%d%d" % (h, e)])
+
+        def shift(k, t0):
+            bank, key = ((T.pC, "pC:t"), (T.pB, "pB:t"))[k]
+            for t in range(t0, t0 + 4):
+                for h in range(2):
+                    n = 16 * k + 2 * t + h
+                    tt(blk(T.part, n, 64), blk(T.mk, t, 64), T.pA[:, 16 * k + 8 * h:16 * k + 8 * h + 8, t:t + 8], A.mult,
+                       ["mk%d" % t, "pA:%d%d0" % (k, h), "pA:%d%d1" % (k, h)], ["part%d" % n])
+                    for e in range(2):
+                        mm(bank[:, e:16:2, 8 * h:8 * h + 8], T.f1[:], blk(T.part, n, 64), t + h + e == 0, t + h + e == 9, ["part%d" % n], [key])
+
+        def back(k):
+            bank, key = ((T.pC, "pC:t"), (T.pB, "pB:t"))[k]
+            op("V", lambda: g.vector.transpose(T.tr[:, 256 * k:256 * k + 256], bank[:, 0:16, :]), [key], ["tr%d" % k])
+
+        def out(k):
+            o = (T.op, T.orr)[k]
+            ts(o[:], T.tr[:, 256 * k:256 * k + 256].indirect(T.tl[:, 0:8]), 2048.0, None, A.add, None, ["tr%d" % k], ["out%d" % k])
+            outs.append(dma("S", (T.yp, T.yr)[k][:], o[:], ["out%d" % k], ()))
+
+        call = {
+            "sx": lambda: tt(T.sx[:], T.mm8[:], T.q4[:, 0::2], A.subtract, ["mm8", "q4"], ["sx"]),
+            "sx7": lambda: ts(T.wp[:], T.sx[:], 7, None, A.bitwise_and, None, ["sx", "bb"], ["sx7", "wp"]),
+            "ra": lambda: ts(T.d1[:], rlo, -2048.0, None, A.add, None, [rk], ["ra"]),
+            "rd": lambda: ts(T.junk[:], dr, BIGH, None, A.mult, None, [rk], ["junk"]),
+            "rb": lambda: tt(T.d2[:], T.d1[:], T.junk[:], A.add, ["ra", "junk"], ["rb"]),
+            "wb": lambda: ts(T.h[:, 0:64], T.lout[:, 128 * s:128 * s + 128:2], 6.0, BIGH, A.is_ge, A.mult, ["lo%d" % s], ["h"]),
+            "rt": lambda: tt(tP, T.h[:, 0:64], dr, A.mult, ["h", rk], ["pV:t"]),
+            "ro": ro,
+        }
+        for k in range(2):
+            call["mk%d" % k] = lambda k=k: masks(4 * k)
+            call["back%d" % k] = lambda k=k: back(k)
+            call["out%d" % k] = lambda k=k: out(k)
+            for b in range(2):
+                call["sf%d%d" % (k, b)] = lambda k=k, b=b: shift(k, 4 * b)
         return call
 
     def run(order, call):
@@ -470,53 +541,18 @@ def rank_program(g, core, T, topo):
                 call[n]()
 
     send_r(1)
-    run(FIRST, near_calls(0))
+    near = near_calls(0)
+    run(FIRST, near)
     for s in range(ST):
         call = step_calls(s)
+        late = {n: near.get(n, lambda: None) for n in LATE}
         if s + 1 < ST:
-            call.update(near_calls(s + 1))
-        run(ORDER, call)
-
-    name[0] = "tail"
-    s = ST - 1
-    rlo, dr = blk(T.rf, s, 128, 0, 64), blk(T.rf, s, 128, 64, 128)
-    C7 = T.pV[:, 128:256]
-    ts(T.h[:, 0:64], T.lout[:, 128 * s:128 * s + 128:2], 6.0, BIGH, A.is_ge, A.mult, ["lo%d" % s], ["h"])
-    tt(T.sx[:], T.mm8[:], T.q4[:, 0::2], A.subtract, ["mm8", "q4"], ["sx"])
-    ts(T.pk[:], T.pout[:, 16 * s:16 * s + 16, 1:9], 2048.0, 4096.0, A.add, A.mult, ["po0%d" % s, "po1%d" % s], ["pk"])
-    tt(tP, T.h[:, 0:64], dr, A.mult, ["h"], ["pV:t"])
-    ts(T.d2[:], dr, BIGH, None, A.mult, None, [], ["d2"])
-    for b in range(3):
-        ts(T.bits[:, 64 * b:64 * b + 64], T.sx[:], b, 1, A.arith_shift_right, A.bitwise_and, ["sx"], ["bits%d" % b])
-    tt(T.d1[:], rlo, T.d2[:], A.add, ["d2"], ["d1"])
-    tt(T.pV[:, 128:192], rlo, tP, A.add, ["pV:t"], ["pV:d1"])
-    tt(T.pV[:, 192:256], T.d1[:], tP, A.subtract, ["d1", "pV:t"], ["pV:d2"])
-    cur, ck, oth, ok = T.xa, "xa", T.xb, "xb"
-    for e in range(2):
-        tt(cur[:, :, 8 * e:8 * e + 8], T.pk[:], C7, A.add, ["pk", "pV:d1", "pV:d2"], [ck + str(e)])
-    for b in range(3):
-        k = 1 << b
-        tt(T.pV[:, 0:128], cur[:, :, k:k + 8], cur[:, :, 0:8], A.subtract, [ck + "0", ck + "1"], ["pV:t", "pV:tr"])
-        for h in range(2):
-            tt(T.pV[:, 256 + 64 * h:320 + 64 * h], T.pV[:, 64 * h:64 * h + 64], T.bits[:, 64 * b:64 * b + 64], A.mult,
-               ["pV:t", "bits%d" % b], ["pV:m2" if h else "pV:m1"])
-        if b < 2:
-            for e in range(2):
-                tt(oth[:, :, 8 * e:8 * e + 8], cur[:, :, 0:8], T.pV[:, 256:384], A.add, [ck + "0", "pV:m1", "pV:m2"], [ok + str(e)])
-            cur, ck, oth, ok = oth, ok, cur, ck
+            near = near_calls(s + 1)
+            call.update(near)
         else:
-            for e in range(2):
-                for h in range(2):
-                    tt(T.dup[:, e::2, 8 * h:8 * h + 8], cur[:, 8 * h:8 * h + 8, 0:8], T.pV[:, 256 + 64 * h:320 + 64 * h], A.add,
-                       [ck + "0", "pV:m1", "pV:m2"], ["fin%d%d" % (e, h)])
-    op("V", lambda: g.vector.transpose(T.tr[:], T.dup[:]), ["fin00", "fin01", "fin10", "fin11"], ["tr"])
-    cp(T.wi[:], T.tr[:, :].indirect(T.tl[:, 0:8]), ["tr"], ["wi"])
-    ts(T.hi3[:], T.wi[:], 12, None, A.arith_shift_right, None, ["wi"], ["hi3"])
-    ts(T.lo3[:], T.wi[:], 4095, None, A.bitwise_and, None, ["wi"], ["lo3"])
-    cp(T.op[:], T.hi3[:], ["hi3"], ["op"])
-    outs.append(dma("Y", T.yp[:], T.op[:], ["op"], ()))
-    cp(T.orr[:], T.lo3[:], ["lo3"], ["orr"])
-    outs.append(dma("S", T.yr[:], T.orr[:], ["orr"], ()))
+            call.update(turn_calls(s))
+        call.update(late)
+        run(ORDER if s + 1 < ST else LAST, call)
 
     count = {q: 0 for q in queue}
     for o in ops:

from concourse.mybir import AluOpType, ActivationFunctionType
from concourse.bass import DstId, RemoteDMATransfer

ST, HOP, NR = 8, 3, 8
F32, BF, F16, I32, U16 = "float32", "bfloat16", "float16", "int32", "uint16"
CH = (("S", 0, 8), ("V", 8, 13), ("S", 13, 16), ("S", 16, 24), ("S", 24, 29), ("S", 29, 32))
CH0 = (2,)
CV = (("S", 0, 16), ("S", 16, 32), ("S", 32, 48), ("V", 48, 64))
ORDER = ("s1 sl af wp qb xx thr zn keep bb dl sy dp t t8 thrb yoff y hf pl pa wr plu poff v0 zd u v1 zr zsend v3 q4 ph fd0 v2 item phu h fd1 far "
         "fa0 qi fa2 tr n16 init fr rlow flag uoff r8 fa1 jn prod sh scat fa3 sm d1 lo lsend fsa fsb nw g1 g2 d2 sa2 zt1 lf zt0 m1 m2 g0 sz sa1 cnt "
         "x2 sa0 g3 sm2 sa3 po x0 sm0 x1 x3 sm1 g4 g5 x4 sa4 rsend lab x5 sm3 sa5 sm4 sm5 sg").split()
FIRST = "zz init lab sg zt0 zt1 sz g0 g1 g2 sa1 x1 sm1 g3 sa0 sa2 x0 sm0 x2 sm2 g4 sa3 x3 sm3 g5 sa4 x4 sm4 sa5 x5 sm5 th".split()
LAST = ("s1 xx zn ra qb thr sl dl keep t8 wp wr bb sy dp t q4 yoff thrb y af pl plu ph h poff u v0 n16 hf tr zd far v1 v2 fd0 v3 fd1 pa phu rd "
        "qi rlow flag fr zr fa2 prod zsend r8 fa0 item uoff scat d1 lo sh sx wb sm sx7 fa1 fsa fa3 fsb rt nw rb lf mk0 m1 d2 ro m2 mk1 po "
        "sf10 sf00 sf01 sf11 back0 back1 out0 out1").split()
LATE = "xx qb af thr sl dp dl zn".split()


def _sb(shape, d):
    return ("sbuf", [128] + list(shape), d)


SCRATCH = {
    "tab": _sb([4096], BF), "a": _sb([2048], BF), "mx": _sb([2048], BF), "zin": _sb([256 * 8], BF), "zp": _sb([8], U16), "zq": _sb([8], U16),
    "prh": _sb([128], F16), "e0": _sb([144], F16), "e1": _sb([144], F16), "v": _sb([1024], BF), "mf": _sb([64, 16], BF),
    "pli": _sb([128], I32), "pri": _sb([128], I32), "thi": _sb([4], I32),
    "zout": _sb([128 * 8], BF), "dd": _sb([128], BF), "lin": _sb([128 * 8], BF), "lout": _sb([128 * 8], BF), "jin": _sb([64 * 8], I32), "jout": _sb([64 * 8], I32),
    "pin": _sb([16 * 8, 10], F16), "pout": _sb([16 * 8, 10], F16), "sl": _sb([16, 10], F16), "roff": _sb([128 * 8], U16), "rf": _sb([128 * 8], F32),
    "ai": _sb([144], I32), "ip": _sb([4], I32), "pm": _sb([8], I32), "col": _sb([8], F32), "ti": _sb([144], I32), "lab0": _sb([128], BF),
    "za": _sb([144], BF), "zm": _sb([144], BF), "zu": _sb([144], BF), "idb": _sb([128], BF), "idn": _sb([128], BF), "idh": _sb([128], BF),
    "id8": _sb([128], BF), "id8n": _sb([128], BF), "idq": _sb([128], BF), "idqn": _sb([128], BF),
    "f1": _sb([128], F16), "f1n": _sb([128], F16), "fh": _sb([128], F16), "fhn": _sb([128], F16), "bones": _sb([128], F32),
    "off": _sb([144], BF), "c2": _sb([128], BF), "cq": _sb([128], BF), "cu": _sb([8], BF), "c1": _sb([128], BF), "low": _sb([128], F32),
    "bc128": _sb([8], U16), "bc64": _sb([8], U16), "bc8": _sb([8], U16), "tl": _sb([8], U16), "negi": _sb([8], F32), "mm8": _sb([64], F32),
    "pk": _sb([128], F32), "dup": _sb([16, 16], F32), "tr": _sb([512], F32), "wi": _sb([128], I32), "hi3": _sb([16, 8], I32), "lo3": _sb([16, 8], I32),
    "s1": _sb([136], F32), "keep": _sb([128], BF), "wp": _sb([64], I32), "bb": _sb([64], I32), "t8": _sb([8], F32), "h": _sb([128], BF),
    "thrb": _sb([128], F32), "poff": _sb([64], U16), "sy": _sb([128], F32), "yoff": _sb([8], U16), "y": _sb([128], BF),
    "wr": _sb([128], I32), "q4": _sb([128], I32), "flag": _sb([128], BF), "far": _sb([128], BF), "n16": _sb([128], BF),
    "qi": _sb([8], I32), "fr": _sb([8], F32), "uoff": _sb([8], U16), "item": _sb([128], BF),
    "prod": _sb([64], I32), "sh": _sb([64], I32), "sm": _sb([64], I32), "nw": _sb([64], I32),
    "pl_": _sb([64], F32), "ph": _sb([64], F32), "plu": _sb([64], F32), "phu": _sb([64], F32), "pa": _sb([64], F32),
    "d1": _sb([64], F32), "d2": _sb([64], F32), "lf": _sb([64], F32), "junk": _sb([64], F32),
    "cnt": _sb([4], F32), "af": _sb([4], F32), "qb": _sb([8], BF), "xx": _sb([4], F32), "thr": _sb([4], F32), "th2": _sb([4], F32),
    "sx": _sb([64], I32), "mk": _sb([512], BF), "part": _sb([2048], F16),
    "op": _sb([128], F32), "orr": _sb([128], F32),
    "pK": ("psum", [128, 512], F32), "pA": ("psum", [128, 32, 16], F32), "pB": ("psum", [128, 32, 16], F32), "pS": ("psum", [128, 512], F32),
    "pC": ("psum", [128, 32, 16], F32), "pD": ("psum", [128, 32, 16], F32), "pX": ("psum", [128, 512], F32), "pV": ("psum", [128, 512], F32),
}
NDMA = 12
SEMAPHORES = (["cV", "cS", "cP", "cG", "sent"] + ["dm%d" % k for k in range(NDMA)]
              + ["%s%d" % (n, s) for n in ("az", "al", "ap", "ar") for s in range(1, 8)])
BIGH = 2.0 ** 23


def rank_program(g, core, T, topo):
    rank = T.rank_of(core)
    if rank is None:
        return
    A = AluOpType
    ACT = ActivationFunctionType
    queue = {"V": g.vector, "S": g.scalar, "P": g.tensor, "G": g, "Y": g.sync}
    ops = []
    writer, readers, banks = {}, {}, {}
    clock = {q: {} for q in queue}
    ndma = [0]
    name = [""]

    def need(q, dep, waits):
        if isinstance(dep, tuple):
            if dep not in clock[q]:
                clock[q][dep] = True
                waits.append(dep)
            return
        o = ops[dep]
        if o["q"] == "P" and q == "P":
            return
        if clock[q].get(o["q"], -1) >= dep:
            return
        waits.append(dep)
        o["used"] = True
        for k, val in o["clock"].items():
            if isinstance(k, tuple):
                clock[q][k] = True
            elif clock[q].get(k, -1) < val:
                clock[q][k] = val
        clock[q][o["q"]] = dep

    def op(q, fn, r=(), w=(), kind="c"):
        deps = []
        for k in r:
            deps.append(writer[k])
        for k in w:
            if k in writer:
                deps.append(writer[k])
            deps.extend(readers.get(k, []))
        bk = set(k.split(":")[0] for k in list(r) + list(w) if ":" in k)
        for b in bk:
            for e, i in banks.get(b, {}).items():
                if e != q:
                    deps.append(i)
        waits = []
        for d in sorted([d for d in deps if not isinstance(d, tuple)], reverse=True) + [d for d in deps if isinstance(d, tuple)]:
            need(q, d, waits)
        idx = len(ops)
        tok = idx
        if kind == "dma":
            tok = ("dm%d" % ndma[0], 16)
            ndma[0] += 1
        ops.append({"q": q, "fn": fn, "waits": waits, "kind": kind, "used": False, "clock": dict(clock[q]), "tok": tok, "name": name[0], "r": r, "w": w})
        if kind != "send":
            for k in r:
                readers.setdefault(k, []).append(tok)
        for k in w:
            writer[k] = tok
            readers[k] = []
        for b in bk:
            banks.setdefault(b, {})[q] = idx
        return tok

    def tt(out, a, b, o, r, w):
        op("V", lambda: g.vector.tensor_tensor(out, a, b, o), r, w)

    def ts(out, a, s1, s2, o0, o1, r, w):
        if o1 is None:
            op("V", lambda: g.vector.tensor_scalar(out, a, s1, None, o0), r, w)
        else:
            op("V", lambda: g.vector.tensor_scalar(out, a, s1, s2, o0, o1), r, w)

    def cp(out, a, r, w):
        op("V", lambda: g.vector.tensor_copy(out, a), r, w)

    def scan(out, d0, d1, init, o0, o1, r, w):
        op("V", lambda: g.vector.tensor_tensor_scan(out, d0, d1, init, o0, o1), r, w)

    def ms(ap, c, w):
        op("V", lambda: g.vector.memset(ap, c), (), w)

    def mm(out, l, rh, st, sp, r, w):
        if st and w[0].startswith("pS:"):
            w = w + ["open"]
        op("P", lambda: g.tensor.matmul(out, l, rh, st, sp), r, w)

    def act(out, a, f, r, w, scale=1.0, bias=0.0):
        op("S", lambda: g.scalar.activation(out, a, f, bias=bias, scale=scale), r, w)

    def dma(q, out, a, r, w):
        return op(q, lambda: queue[q].dma_start(out, a), r, w, kind="dma")

    sent = [0]

    def send(dst_rank, pairs, sem, r):
        dst = T.cores[dst_rank]
        rid, pid, _ = topo.addr(dst)
        eng = topo.engines(core, dst)
        sent[0] += len(eng)
        if len(pairs) == 1:
            op("G", lambda: g.remote_dma(pairs[0][0], pairs[0][1], T.sem[sem], T.sem.sent, pid, rid, topo.mask(core, dst)), r, (), kind="send")
            return
        n = len(eng) // len(pairs)
        trs = [RemoteDMATransfer(dst_ids=[DstId(rid=rid, pnc=pid)], dma_engine_mask=sum(1 << e for e in eng[n * k:n * k + n]),
                                 remote_sem=T.sem[sem], src=a, dst=out) for k, (out, a) in enumerate(pairs)]
        op("G", lambda: g.remote_dma_fused(trs, local_sem=T.sem.sent), r, (), kind="send")

    def lands(src_rank, calls):
        return calls * len(topo.engines(T.cores[src_rank], core))

    def blk(t, s, n, a=0, b=None):
        return t[:, n * s + a:n * s + (n if b is None else b)]

    def zin(s, a=0, b=128):
        return blk(T.zin, s, 256, a, b)

    def pv(t, s, h, k):
        return t[:, 16 * s + 8 * h:16 * s + 8 * h + 8, k:k + 8]

    prev, nxt = (rank - HOP) % NR, (rank + HOP) % NR
    for s in range(1, ST):
        writer["z%d" % s] = ("az%d" % s, lands(prev, 1))
        writer["l%d" % s] = writer["j%d" % s] = ("al%d" % s, lands(prev, 1))
        writer["p%d" % s] = ("ap%d" % s, lands(prev, 1))
        writer["ro%d" % s] = writer["rf%d" % s] = ("ar%d" % s, lands((rank - HOP * s) % NR, 2))

    dma("Y", T.pri[:], T.pr[:], (), ["pri"])
    dma("S", T.pli[:], T.pl[:], (), ["pli"])
    dma("Y", zin(0), T.z0[:], (), ["zn0"])
    dma("Y", T.tab[:], T.xt[:], (), ["tab"])
    dma("S", T.thi[:, 0:1], T.th[:], (), ["thi"])

    op("G", lambda: g.iota(T.ip[:, 0:1], [[0, 1]], 0, 1), (), ["ip"])
    op("G", lambda: g.iota(T.ai[:], [[1, 144]], 0, 0), (), ["ai"])
    op("G", lambda: g.iota(T.lab0[:], [[0, 8], [1, 8], [8, 2]], -2, 0, allow_small_or_imprecise_dtypes=True), (), ["lab0"])
    op("G", lambda: g.iota(T.sx[:], [[0, 8], [1, 8]], 7, 0), (), ["sx"])
    op("G", lambda: g.iota(T.ti[:, 128:144], [[0, 2], [-1, 8]], 0, 0), (), ["tib"])
    for t, c in (("c2", -2.0), ("cq", -0.25), ("cu", -15.5 / 32), ("c1", -1.0), ("low", 0.0), ("junk", 0.0)):
        ms(T[t][:], c, [t])
    ms(T.s1[:, 0:8], -1.0e9, ["s1"])
    ms(T.af[:, 0:1], 2048.0, ["af"])
    for k, m in enumerate((31, 112, 8, 15, 7)):
        ts(T.pm[:, k:k + 1], T.ip[:, 0:1], m, None, A.bitwise_and, None, ["ip"], ["pm%d" % k])
    cp(T.col[:, 5:6], T.ip[:, 0:1], ["ip"], ["col5"])
    cp(T.col[:, 0:1], T.pm[:, 0:1], ["pm0"], ["col0"])
    cp(T.col[:, 1:2], T.pm[:, 1:2], ["pm1"], ["col1"])
    ts(T.col[:, 2:3], T.pm[:, 1:2], 15.0, None, A.add, None, ["pm1"], ["col2"])
    ts(T.col[:, 3:4], T.pm[:, 2:3], 2.0, 16.0, A.mult, A.add, ["pm2"], ["col3"])
    cp(T.col[:, 4:5], T.pm[:, 3:4], ["pm3"], ["col4"])
    ts(T.col[:, 6:7], T.pm[:, 2:3], -32.0, T.col[:, 5:6], A.mult, A.add, ["pm2", "col5"], ["col6"])
    ts(T.col[:, 7:8], T.pm[:, 2:3], 32.0, T.col[:, 5:6], A.mult, A.add, ["pm2", "col5"], ["col7"])
    ts(T.xx[:, 1:2], T.pm[:, 2:3], 0.125, None, A.mult, None, ["pm2"], ["xx1"])
    ts(T.xx[:, 3:4], T.pm[:, 3:4], 8.0, None, A.mult, None, ["pm3"], ["xx3"])
    ts(T.idb[:], T.ai[:, 0:128], T.col[:, 5:6], None, A.is_equal, None, ["ai", "col5"], ["idb"])
    ts(T.e0[:], T.ai[:], -8.0, T.col[:, 6:7], A.add, A.is_equal, ["ai", "col6"], ["e0"])
    ts(T.e1[:], T.ai[:], 248.0, T.col[:, 7:8], A.add, A.is_equal, ["ai", "col7"], ["e1"])
    ts(T.za[:], T.ai[:], T.col[:, 2:3], 16.0, A.is_equal, A.mult, ["ai", "col2"], ["za"])
    ts(T.xx[:, 2:3], T.pm[:, 4:5], 16.0, T.xx[:, 1:2], A.mult, A.add, ["pm4", "xx1"], ["xx2"])
    ts(T.tl[:], T.ai[:, 0:8], 32.0, T.col[:, 0:1], A.mult, A.add, ["ai", "col0"], ["tl"])
    cp(T.pout[:, :, 9], T.low[:], ["low"], ["pz"])
    for t, src, wgt in (("zm", "za", -2.0), ("zu", "za", 1.0 / 512), ("idn", "idb", -1.0), ("idh", "idb", 0.5), ("id8", "idb", 8.0),
                        ("id8n", "idb", -8.0), ("idq", "idb", 0.125), ("idqn", "idb", -0.125)):
        act(T[t][:], T[src][:], ACT.Copy, [src], [t], wgt)

    ts(T.prh[:], T.pri[:], -2048.0, None, A.add, None, ["pri"], ["prh"])
    for h in range(2):
        for b in range(2):
            for c in range(4):
                mm(T.pX[:, 64 * h + c:64 * h + 64:4], T["e%d" % h][:, 8 - 8 * (b - h):136 - 8 * (b - h)], T.prh[:, 32 * c + 16 * b:32 * c + 16 * b + 16],
                   h + b + c == 0, h + b + c == 5, ["e%d" % h, "prh"], ["pX:ro"])
    ts(T.pk[:], T.pli[:], 4096.0, None, A.mult, None, ["pli"], ["pk"])
    ts(T.ti[:, 0:128], T.ai[:, 0:128], 4, None, A.arith_shift_right, None, ["ai"], ["ti"])
    ts(T.q4[:], T.ai[:, 0:128], 112, None, A.bitwise_and, None, ["ai"], ["q4"])
    for e in range(2):
        tt(T.dup[:, e::2, :], T.pk[:], T.pri[:], A.add, ["pk", "pri"], ["dup%d" % e])
    ts(T.roff[:, 0:128], T.pX[:, 0:128], 2048.0, None, A.add, None, ["pX:ro"], ["ro0"])
    ts(T.off[:], T.ti[:], 2.0 ** 18, None, A.mult, None, ["ti", "tib"], ["off"])
    op("V", lambda: g.vector.transpose(T.tr[:, 0:256], T.dup[:]), ["dup0", "dup1"], ["tr0"])
    ts(T.bones[:], T.q4[:], T.col[:, 1:2], None, A.is_equal, None, ["q4", "col1"], ["bones"])
    ts(T.zp[:], T.ai[:, 0:8], 2.0, T.xx[:, 2:3], A.mult, A.add, ["ai", "xx2"], ["zp"])
    ts(T.zq[:], T.ai[:, 0:8], T.xx[:, 3:4], None, A.add, None, ["ai", "xx3"], ["zq"])
    cp(T.wi[:], T.tr[:, 0:256].indirect(T.tl[:, 0:8]), ["tr0", "tl"], ["wi"])
    for t, wgt in (("f1", 1.0), ("f1n", -1.0), ("fh", 0.5), ("fhn", -0.5)):
        ts(T[t][:], T.idb[:], wgt, None, A.mult, None, ["idb"], [t])
    ts(T.lo3[:], T.wi[:], 4095, None, A.bitwise_and, None, ["wi"], ["lo3"])
    ts(T.hi3[:], T.wi[:], 12, None, A.arith_shift_right, None, ["wi"], ["hi3"])
    cp(T.pin[:, 0:16, 9], T.junk[:, 0:16], ["junk"], ["p0z"])
    cp(T.sl[:, :, 8], T.junk[:, 0:16], ["junk"], ["slz"])
    tt(T.d1[:], T.lo3[:, 1::2, :], T.lo3[:, 0::2, :], A.subtract, ["lo3"], ["d1"])
    cp(T.rf[:, 0:64], T.lo3[:, 0::2, :], ["lo3"], ["rf0a"])
    for h in range(2):
        ts(pv(T.pin, 0, h, 1), T.hi3[:, h::2, :], -2048.0, None, A.add, None, ["hi3"], ["p0a%d" % h])
        ts(T.pin[:, 8 * h:8 * h + 8, 0], T.hi3[:, h::2, 7], -2048.0, None, A.add, None, ["hi3", "p0z"], ["p0b%d" % h])
    ts(T.rf[:, 64:128], T.d1[:], 1.0 / BIGH, None, A.mult, None, ["d1"], ["rf0"])
    writer["p0"] = writer["p0b1"]
    ts(T.bc128[:], T.ai[:, 0:8], 16.0, 16.0, A.mult, A.add, ["ai"], ["bc128"])
    ts(T.bc64[:], T.ai[:, 0:8], 32.0, T.col[:, 3:4], A.mult, A.add, ["ai", "col3"], ["bc64"])
    cp(T.bc8[:], T.ai[:, 0:8], ["ai"], ["bc8"])
    ts(T.negi[:], T.ai[:, 0:8], -16.0, T.col[:, 4:5], A.mult, A.subtract, ["ai", "col4"], ["negi"])
    ts(T.jin[:, 0:64], T.sx[:], 7, None, A.bitwise_and, None, ["sx"], ["j0"])
    cp(T.lin[:, 0:128], T.lab0[:], ["lab0"], ["l0"])
    ts(T.mm8[:], T.sx[:], 16.0, None, A.add, None, ["sx"], ["mm8"])

    def sel(t, r):
        return t[:, 15 - r:143 - r]

    K, SZ = T.pK[:, 0:128], T.pK[:, 128:136]
    HF, Fp, AP_, DL = T.pS[:, 128:256], T.pS[:, 256:320], T.pS[:, 320:321], T.pS[:, 384:512]
    U, R8, DP, SG = T.pX[:, 0:8], T.pX[:, 128:256], T.pX[:, 256:320], T.pX[:, 320:384]
    tP, tR, D1, D2, M1, M2 = (T.pV[:, 64 * k:64 * k + 64] for k in range(6))
    HH = T.pV[:, 384:512]
    tiles = ((T.pA, "pA:t"), (T.pB, "pB:t"))
    ftiles = ((T.pC, "pC:t"), (T.pD, "pD:t"))
    win = T.tab[:, :]
    outs = []

    def gather(q, out, off, r, w):
        if q == "V":
            cp(out, win.indirect(off), ["tab", r], [w])
        else:
            act(out, win.indirect(off), ACT.Copy, ["tab", r], [w])

    def send_r(s):
        d = (rank + HOP * s) % NR
        send(d, [(blk(T.roff, s, 128), blk(T.roff, 0, 128))], "ar%d" % s, ["ro0"])
        send(d, [(blk(T.rf, s, 128), blk(T.rf, 0, 128))], "ar%d" % s, ["rf0a", "rf0"])

    def near_calls(s):
        zk, lk, pk_ = "z%d" % s, "l%d" % s, "p%d" % s

        def right(k):
            q, lo_, hi_ = CH[k]
            gather("V" if s == 0 and k in CH0 else q, T.a[:, 64 * lo_:64 * hi_], blk(T.roff, s, 128, 4 * lo_, 4 * hi_), "ro%d" % s, "a%d" % k)

        def init():
            mm(T.pK[:, 0:144], T.idb[:], T.off[:], True, False, ["idb", "off"], ["pK:k"])
            mm(K, T.idb[:], T.c2[:], False, False, ["c2"], ["pK:k"])

        def ztile(hh):
            for m in range(8):
                mm(tiles[hh][0][:, :, m::8], T.idb[:], zin(s, 128 + 64 * hh, 192 + 64 * hh), True, True, ["idb", zk], [tiles[hh][1]])

        def big(k):
            _, lo_, hi_ = CH[k]
            t = tiles[lo_ // 8 % 2]
            tt(T.mx[:, 64 * lo_:64 * hi_], T.a[:, 64 * lo_:64 * hi_], t[0][:, 4 * (lo_ % 8):4 * ((hi_ - 1) % 8 + 1), :], A.max,
               ["a%d" % k, t[1]], ["mx%d" % k])

        def sums(k, t, w_, key, stop):
            for b in range(CH[k][1], CH[k][2]):
                mm(T.pK[:, b // 16:128:2], sel(T[w_], b % 16), blk(t, b, 64), False, stop and b == CH[k][2] - 1, [key + str(k), w_], ["pK:k"])

        def sz():
            for r in range(16):
                mm(SZ, sel(T.za, r), zin(s, 128 + 8 * r, 136 + 8 * r), False, False, ["za", zk], ["pK:k"])

        def th():
            ts(T.thr[:, 0:1], T.thi[:, 0:1], 1.0, -16.0, A.add, A.mult, ["thi"], ["thr"])
            ts(T.th2[:, 0:1], T.thi[:, 0:1], 1.0 + 32 * 192, -16.0, A.add, A.mult, ["thi"], ["th2"])

        def dp():
            mm(DP, T.f1[:], pv(T.pin, s, 1, 0), True, False, ["f1", pk_], ["pX:dp"])
            mm(DP, T.f1n[:], pv(T.pin, s, 0, 0), False, True, ["f1n", pk_], ["pX:dp"])

        def sg():
            mm(SG, T.idq[:], T.lin[:, 128 * s + 1:128 * s + 128:2], True, False, ["idq", lk], ["pX:sg"])
            mm(SG, T.idqn[:], T.lin[:, 128 * s:128 * s + 128:2], False, True, ["idqn", lk], ["pX:sg"])

        def sl():
            for h in range(2):
                tt(pv(T.sl, 0, h, 0), pv(T.pin, s, h, 1), SG, A.mult, [pk_, "pX:sg", "slz"], ["sl%d" % h])

        def dl():
            b, a_ = T.pS[:, 385:512:2], T.pS[:, 384:512:2]
            terms = [(T.fh, T.pin, s, 0, 1), (T.fh, T.pin, s, 1, 1), (T.fhn, T.pin, s, 0, 2), (T.fhn, T.pin, s, 1, 2),
                     (T.fhn, T.sl, 0, 0, 0), (T.fhn, T.sl, 0, 0, 1), (T.fh, T.sl, 0, 1, 0), (T.fh, T.sl, 0, 1, 1)]
            for k, (w_, t, s_, h, k0) in enumerate(terms):
                mm(b, w_[:], pv(t, s_, h, k0), k == 0, False, ["fh", "fhn", pk_ if k < 4 else "sl%d" % h], ["pS:dl"])
            mm(a_, T.f1[:], pv(T.sl, 0, 0, 0), False, False, ["f1", "sl0"], ["pS:dl"])
            mm(a_, T.f1n[:], pv(T.sl, 0, 1, 0), False, True, ["f1n", "sl1"], ["pS:dl"])

        call = {
            "init": init, "dp": dp, "sg": sg, "sl": sl, "dl": dl,
            "lab": lambda: mm(K, T.idn[:], blk(T.lin, s, 128), False, False, ["idn", lk], ["pK:k"]),
            "sz": sz,
            "zn": lambda: act(zin(s), zin(s, 128, 256).indirect(T.zq[:, 0:8]), ACT.Copy, [zk, "zq"], ["zn%d" % s]),
            "af": lambda: act(T.af[:, 0:1], AP_, ACT.Identity, ["pS:a"], ["af"], bias=2048.0),
            "qb": lambda: act(T.qb[:, 0:1], AP_, ACT.Identity, ["pS:a"], ["qb"], 1.0 / 32, 192 - 15.5 / 32),
            "xx": lambda: act(T.xx[:, 0:1], AP_, ACT.Identity, ["pS:a", "th2"], ["xx"], -16.0, T.th2[:, 0:1]),
            "thr": lambda: act(T.thr[:, 0:1], T.qb[:, 0:1], ACT.Identity, ["qb", "xx"], ["thr"], 512.0, T.xx[:, 0:1]),
        }
        for k in range(len(CH)):
            call["g%d" % k] = lambda k=k: right(k)
            call["x%d" % k] = lambda k=k: big(k)
            call["sa%d" % k] = lambda k=k: sums(k, T.a, "za", "a", False)
            call["sm%d" % k] = lambda k=k: sums(k, T.mx, "zm", "mx", k == len(CH) - 1)
        for h in range(2):
            call["zt%d" % h] = lambda h=h: ztile(h)
        if s == 0:
            for n in ("af", "qb", "xx", "thr", "zn"):
                del call[n]
            call["th"] = th
            call["zz"] = lambda: act(zin(0, 128, 256), zin(0).indirect(T.zp[:, 0:8]), ACT.Copy, ["zn0", "zp"], ["z0"])
        return call

    def step_calls(s):
        last = s == ST - 1
        z, zk, lk, jk, pk_, rk = zin(s), "zn%d" % s, "l%d" % s, "j%d" % s, "p%d" % s, "rf%d" % s
        rlo, dr = blk(T.rf, s, 128, 0, 64), blk(T.rf, s, 128, 64, 128)
        zo = blk(T.zout, s, 128)

        def r8():
            mm(R8, T.idb[:], T.c1[:], True, False, ["c1"], ["pX:r8"])
            mm(R8, T.idb[:], T.n16[:], False, False, ["n16"], ["pX:r8"])
            mm(R8, T.id8[:], T.flag[:], False, False, ["id8", "flag"], ["pX:r8"])
            mm(T.pX[:, 128:256:2], T.id8n[:], T.flag[:, 1::2], False, False, ["id8n", "flag"], ["pX:r8"])
            mm(T.pX[:, 129:256:2], T.id8n[:], T.flag[:, 0::2], False, True, ["flag"], ["pX:r8"])

        def u():
            mm(U, T.idb[:], T.cu[:], True, False, ["cu"], ["pX:u"])
            for r in range(16):
                mm(U, sel(T.zu, r), T.y[:, r::16], False, r == 15, ["zu", "y"], ["pX:u"])

        def hf():
            mm(HF, T.idh[:], T.y[:], True, False, ["idh", "y"], ["pS:h"])
            mm(HF, T.idh[:], z, False, False, [zk], ["pS:h"])
            mm(HF, T.idb[:], T.cq[:], False, True, ["cq"], ["pS:h"])

        def zsend():
            if last:
                outs.append(dma("Y", T.yz[:], zo, ["zo%d" % s], ()))
            else:
                send(nxt, [(zin(s + 1, 128, 256), zo)], "az%d" % (s + 1), ["zo%d" % s])

        def fd(hh):
            t, key = ftiles[hh]
            for m in range(8):
                mm(t[:, m::8, :], T.idn[:], T.y[:, 64 * hh:64 * hh + 64], m == 0, False, ["y"], [key])
            mm(t[:], T.idb[:], T.v[:, 512 * hh:512 * hh + 512], False, True,
               ["v%d" % k for k, c in enumerate(CV) if c[1] < 32 * hh + 32 and c[2] > 32 * hh], [key])

        def fa(k):
            hh, r0 = k % 2, 8 * (k // 2)
            act(T.mf[:, 32 * hh:32 * hh + 32, r0:r0 + 8], ftiles[hh][0][:, :, r0:r0 + 8], ACT.Abs, [ftiles[hh][1]], ["mf%d" % k], 0.5)

        def fs(b):
            for r in range(8 * b, 8 * b + 8):
                mm(Fp, sel(T.zm, r), T.mf[:, :, r], r == 0, r == 15, ["mf%d" % (2 * b), "mf%d" % (2 * b + 1)], ["pS:f", "open"])

        def lsend():
            send(nxt, [(blk(T.lin, s + 1, 128), blk(T.lout, s, 128)), (blk(T.jin, s + 1, 64), blk(T.jout, s, 64))],
                 "al%d" % (s + 1), ["lo%d" % s, "jn%d" % s])

        def scat():
            cp(win.indirect(T.uoff[:, 0:8]), T.item[:], ["uoff", "item"], ["tab"])
            if last:
                outs.append(dma("Y", T.yx[:], T.tab[:], ["tab"], ()))

        def po():
            for h, (x, xk, m, mk) in enumerate(((T.pl_, "pl", 4, "pV:m1"), (T.ph, "ph", 5, "pV:m2"))):
                if last:
                    for e in range(2):
                        tt(T.pA[:, 8 * h:8 * h + 8, 8 * e:8 * e + 8], x[:], T.pV[:, 64 * m:64 * m + 64], A.add, [xk, mk], ["pA:0%d%d" % (h, e)])
                    continue
                tt(pv(T.pout, s, h, 1), x[:], T.pV[:, 64 * m:64 * m + 64], A.add, [xk, mk, "pz"], ["po%d%d" % (h, s)])
                tt(T.pout[:, 16 * s + 8 * h:16 * s + 8 * h + 8, 0], x[:, 7::8], T.pV[:, 64 * m + 7:64 * m + 64:8], A.add, [xk, mk], ["pw%d%d" % (h, s)])
            if not last:
                send(nxt, [(T.pin[:, 16 * s + 16:16 * s + 32, :], T.pout[:, 16 * s:16 * s + 16, :])], "ap%d" % (s + 1),
                     ["po0%d" % s, "po1%d" % s, "pw0%d" % s, "pw1%d" % s])

        def cnt():
            op("S", lambda: g.scalar.activation(T.junk[:], T.lf[:], ACT.Copy, accum_out=T.cnt[:, 0:1]), ["lf"], ["cnt", "junk"])
            mm(AP_, T.bones[:], T.cnt[:, 0:1], True, True, ["bones", "cnt"], ["pS:a"])

        call = {
            "s1": lambda: scan(T.s1[:, 1:129], T.low[:], K, -1.0e9, A.add, A.max, ["low", "pK:k"], ["s1"]),
            "keep": lambda: tt(T.keep[:], K, T.s1[:, 0:128], A.is_lt, ["pK:k", "s1"], ["keep"]),
            "sy": lambda: scan(T.sy[:], T.keep[:], DL, 0.0, A.mult, A.add, ["keep", "pS:dl"], ["sy"]),
            "yoff": lambda: ts(T.yoff[:], T.sy[:, 15::16], 2048.0, None, A.add, None, ["sy"], ["yoff"]),
            "y": lambda: act(T.y[:], win.indirect(T.yoff[:, 0:8]), ACT.Copy, ["tab", "yoff"], ["y"]),
            "hf": hf, "zsend": zsend, "u": u,
            "zd": lambda: tt(T.dd[:], win.indirect(T.yoff[:, 0:8]), z, A.subtract, ["tab", "yoff", zk], ["dd"]),
            "zr": lambda: act(zo, T.dd[:] if last else T.dd[:, :].indirect(T.zp[:, 0:8]), ACT.Abs, ["dd", "zp"], ["zo%d" % s]),
            "wp": lambda: tt(T.wp[:], T.s1[:, :].indirect(T.bc64[:, 0:4]), blk(T.jin, s, 64), A.add, ["s1", "bc64", jk], ["wp"]),
            "bb": lambda: ts(T.bb[:], T.wp[:], 3, 1, A.arith_shift_right, A.bitwise_and, ["wp"], ["bb"]),
            "t": lambda: tt(tP, T.bb[:], DP, A.mult, ["bb", "pX:dp"], ["pV:t"]),
            "pl": lambda: tt(T.pl_[:], pv(T.pin, s, 0, 0), tP, A.add, [pk_, "pV:t"], ["pl"]),
            "ph": lambda: tt(T.ph[:], pv(T.pin, s, 1, 0), tP, A.subtract, [pk_, "pV:t"], ["ph"]),
            "poff": lambda: ts(T.poff[:], T.pl_[:], 2048.0, None, A.add, None, ["pl"], ["poff"]),
            "t8": lambda: act(T.t8[:], SZ, ACT.Identity, ["pK:k", "thr"], ["t8"], -1.0, T.thr[:, 0:1]),
            "wr": lambda: tt(T.wr[:], T.s1[:, :].indirect(T.bc128[:, 0:8]), blk(T.lin, s, 128), A.add, ["s1", "bc128", lk], ["wr"]),
            "q4": lambda: ts(T.q4[:], T.wr[:], 15, None, A.bitwise_and, None, ["wr"], ["q4"]),
            "jn": lambda: ts(blk(T.jout, s, 64), T.wr[:, 0::2], 7, None, A.bitwise_and, None, ["wr"], ["jn%d" % s]),
            "h": lambda: ts(HH, T.q4[:], 7.0, BIGH, A.is_ge, A.mult, ["q4"], ["pV:h"]),
            "n16": lambda: ts(T.n16[:], T.q4[:], 15.0, -16.0, A.is_equal, A.mult, ["q4"], ["n16"]),
            "thrb": lambda: act(T.thrb[:], T.t8[:, :].indirect(T.bc8[:, 0:8]), ACT.Copy, ["t8", "bc8"], ["thrb"]),
            "far": lambda: tt(T.far[:], K, T.thrb[:], A.is_le, ["pK:k", "thrb"], ["far"]),
            "flag": lambda: tt(T.flag[:], T.far[:], HH, A.is_gt, ["far", "pV:h"], ["flag"]),
            "r8": r8, "lsend": lsend,
            "lo": lambda: tt(blk(T.lout, s, 128), T.q4[:], R8, A.add, ["q4", "pX:r8"], ["lo%d" % s]),
            "qi": lambda: tt(T.qi[:], U, T.negi[:], A.add, ["pX:u", "negi"], ["qi"]),
            "fr": lambda: tt(T.fr[:], U, T.qi[:], A.subtract, ["pX:u", "qi"], ["fr"]),
            "uoff": lambda: ts(T.uoff[:], T.fr[:], 32.0, 15.5, A.mult, A.add, ["fr"], ["uoff"]),
            "item": lambda: ts(T.item[:], HF, 12582912.0, 12582912.0, A.add, A.subtract, ["pS:h"], ["item"]),
            "scat": scat, "fsa": lambda: fs(0), "fsb": lambda: fs(1),
            "plu": lambda: act(T.plu[:], T.pl_[:], ACT.Identity, ["pl"], ["plu"], bias=2048.0),
            "phu": lambda: act(T.phu[:], T.ph[:], ACT.Identity, ["ph"], ["phu"], bias=2048.0),
            "pa": lambda: act(T.pa[:], T.pl_[:], ACT.Identity, ["pl", "af"], ["pa"], bias=T.af[:, 0:1]),
            "tr": lambda: tt(tR, T.pV[:, 384:512:2], dr, A.mult, [rk, "pV:h"], ["pV:tr"]),
            "rlow": lambda: tt(tR, rlo, tR, A.add, [rk, "pV:tr"], ["pV:tr"]),
            "d1": lambda: tt(D1, T.ph[:], T.pl_[:], A.subtract, ["ph", "pl"], ["pV:d1"]),
            "prod": lambda: tt(T.prod[:], T.plu[:], tR, A.mult, ["plu", "pV:tr"], ["prod"]),
            "sh": lambda: ts(T.sh[:], T.prod[:], 5, None, A.arith_shift_right, None, ["prod"], ["sh"]),
            "sm": lambda: tt(T.sm[:], T.sh[:], T.pa[:], A.add, ["sh", "pa"], ["sm"]),
            "nw": lambda: ts(T.nw[:], T.sm[:], 4095, None, A.bitwise_and, None, ["sm"], ["nw"]),
            "d2": lambda: tt(D2, T.nw[:], T.phu[:], A.subtract, ["nw", "phu"], ["pV:d2"]),
            "lf": lambda: ts(T.lf[:], Fp, T.thr[:, 0:1], None, A.is_le, None, ["pS:f", "thr"], ["lf"]),
            "m1": lambda: tt(M1, T.lf[:], D1, A.mult, ["pV:d1", "lf"], ["pV:m1"]),
            "m2": lambda: tt(M2, T.lf[:], D2, A.mult, ["pV:d2", "lf"], ["pV:m2"]),
            "po": po, "cnt": cnt,
            "rsend": lambda: s + 2 < ST and send_r(s + 2),
        }
        for k in range(len(CV)):
            call["v%d" % k] = lambda k=k: gather(CV[k][0], T.v[:, 16 * CV[k][1]:16 * CV[k][2]], T.poff[:, CV[k][1]:CV[k][2]], "poff", "v%d" % k)
        for hh in range(2):
            call["fd%d" % hh] = lambda hh=hh: fd(hh)
        for k in range(4):
            call["fa%d" % k] = lambda k=k: fa(k)
        return call

    def turn_calls(s):
        rlo, dr = blk(T.rf, s, 128, 0, 64), blk(T.rf, s, 128, 64, 128)
        rk = "rf%d" % s

        def masks(t0):
            for t in range(t0, t0 + 4):
                ts(blk(T.mk, t, 64), T.wp[:], float(t), None, A.is_equal, None, ["sx7"], ["mk%d" % t])

        def ro():
            for h, (x, xk, o) in enumerate(((T.d1, "ra", A.add), (T.d2, "rb", A.subtract))):
                for e in range(2):
                    tt(T.pA[:, 16 + 8 * h:24 + 8 * h, 8 * e:8 * e + 8], x[:], tP, o, [xk, "pV:t"], ["pA:1%d%d" % (h, e)])

        def shift(k, t0):
            bank, key = ((T.pC, "pC:t"), (T.pB, "pB:t"))[k]
            for t in range(t0, t0 + 4):
                for h in range(2):
                    n = 16 * k + 2 * t + h
                    tt(blk(T.part, n, 64), blk(T.mk, t, 64), T.pA[:, 16 * k + 8 * h:16 * k + 8 * h + 8, t:t + 8], A.mult,
                       ["mk%d" % t, "pA:%d%d0" % (k, h), "pA:%d%d1" % (k, h)], ["part%d" % n])
                    for e in range(2):
                        mm(bank[:, e:16:2, 8 * h:8 * h + 8], T.f1[:], blk(T.part, n, 64), t + h + e == 0, t + h + e == 9, ["part%d" % n], [key])

        def back(k):
            bank, key = ((T.pC, "pC:t"), (T.pB, "pB:t"))[k]
            op("V", lambda: g.vector.transpose(T.tr[:, 256 * k:256 * k + 256], bank[:, 0:16, :]), [key], ["tr%d" % k])

        def out(k):
            o = (T.op, T.orr)[k]
            ts(o[:], T.tr[:, 256 * k:256 * k + 256].indirect(T.tl[:, 0:8]), 2048.0, None, A.add, None, ["tr%d" % k], ["out%d" % k])
            outs.append(dma("S", (T.yp, T.yr)[k][:], o[:], ["out%d" % k], ()))

        call = {
            "sx": lambda: tt(T.sx[:], T.mm8[:], T.q4[:, 0::2], A.subtract, ["mm8", "q4"], ["sx"]),
            "sx7": lambda: ts(T.wp[:], T.sx[:], 7, None, A.bitwise_and, None, ["sx", "bb"], ["sx7", "wp"]),
            "ra": lambda: ts(T.d1[:], rlo, -2048.0, None, A.add, None, [rk], ["ra"]),
            "rd": lambda: ts(T.junk[:], dr, BIGH, None, A.mult, None, [rk], ["junk"]),
            "rb": lambda: tt(T.d2[:], T.d1[:], T.junk[:], A.add, ["ra", "junk"], ["rb"]),
            "wb": lambda: ts(T.h[:, 0:64], T.lout[:, 128 * s:128 * s + 128:2], 6.0, BIGH, A.is_ge, A.mult, ["lo%d" % s], ["h"]),
            "rt": lambda: tt(tP, T.h[:, 0:64], dr, A.mult, ["h", rk], ["pV:t"]),
            "ro": ro,
        }
        for k in range(2):
            call["mk%d" % k] = lambda k=k: masks(4 * k)
            call["back%d" % k] = lambda k=k: back(k)
            call["out%d" % k] = lambda k=k: out(k)
            for b in range(2):
                call["sf%d%d" % (k, b)] = lambda k=k, b=b: shift(k, 4 * b)
        return call

    def run(order, call):
        for n in order:
            if n in call:
                name[0] = n
                call[n]()

    send_r(1)
    near = near_calls(0)
    run(FIRST, near)
    for s in range(ST):
        call = step_calls(s)
        late = {n: near.get(n, lambda: None) for n in LATE}
        if s + 1 < ST:
            near = near_calls(s + 1)
            call.update(near)
        else:
            call.update(turn_calls(s))
        call.update(late)
        run(ORDER if s + 1 < ST else LAST, call)

    count = {q: 0 for q in queue}
    for o in ops:
        if o["kind"] == "c" and o["used"]:
            count[o["q"]] += 1
            o["n"] = count[o["q"]]
    for o in ops:
        e = queue[o["q"]]
        for d in o["waits"]:
            if isinstance(d, tuple):
                e.wait_ge(T.sem[d[0]], d[1])
            else:
                e.wait_ge(T.sem["c" + ops[d]["q"]], ops[d]["n"])
        ins = o["fn"]()
        if o["kind"] == "dma":
            ins.then_inc(T.sem[o["tok"][0]], 16)
        elif o["kind"] == "c" and o["used"]:
            ins.then_inc(T.sem["c" + o["q"]], 1)
    for tok in outs:
        g.wait_ge(T.sem[tok[0]], tok[1])
    g.wait_ge(T.sem.sent, sent[0])
